import numpy as np
import ml_dtypes


def mxq(x, axis, fmt="e4m3"):
    dtype, down = {"e4m3": (ml_dtypes.float8_e4m3fn, 7), "e5m2": (ml_dtypes.float8_e5m2, 14)}[fmt]
    v = np.moveaxis(np.asarray(x, np.float32).astype(ml_dtypes.bfloat16).astype(np.float64), axis, -1)
    blocks = v.reshape(v.shape[:-1] + (-1, 32))
    amax = np.abs(blocks).max(-1, keepdims=True)
    byte = np.maximum(np.where(amax > 0, np.frexp(amax)[1] - 1 + 127, 0) - down, 1)
    scale = np.exp2(byte - 127.0)
    codes = (blocks / scale).astype(np.float32).astype(dtype).astype(np.float64)
    return np.moveaxis((codes * scale).reshape(v.shape), -1, axis)


WIDE = False


def mx_kscale(k):
    if not WIDE:
        return np.ones(k)
    levels = np.array([10, -10, 5, -5, 0])
    if k % 512:
        return np.exp2(np.random.permutation(np.resize(levels, k // 32))).repeat(32)
    a = np.empty((k // 512, 16))
    for p in range(k // 512):
        a[p, :8] = np.random.permutation(np.resize(levels, 8))
        for g in range(8):
            far = levels[np.abs(levels - a[p, g]) >= 10]
            a[p, g + 8] = far[np.random.randint(len(far))]
    return np.exp2(a.ravel()).repeat(32)


def f64(x):
    return np.asarray(x).astype(np.float64)


def striped(idx):
    return np.tile(idx.reshape(-1, 16).T, (8, 1)).astype(np.uint16)


def unstriped(offs):
    return offs[:16].T.reshape(-1).astype(np.int64)


def pack_weight(w):
    k, n = w.shape
    w = f64(np.asarray(w, np.float32).astype(ml_dtypes.bfloat16)).reshape(k // 32, 32, n)
    amax = np.abs(w).max(1)
    byte = np.clip(np.where(amax > 0, np.frexp(amax)[1] - 1 + 127 - 7, 1), 1, 254)
    scaled = (w * np.exp2(127.0 - byte)[:, None, :]).reshape(k, n).astype(np.float32)
    words = np.ascontiguousarray(scaled.reshape(k // 512, 128, 4, n).transpose(0, 1, 3, 2)).astype(ml_dtypes.float8_e4m3fn).view(np.uint8)
    return words, np.ascontiguousarray(byte.astype(np.uint8).reshape(k // 512, 16, n))


def unpack_weight(words, scales):
    g, p, n, _ = words.shape
    vals = np.ascontiguousarray(words).view(ml_dtypes.float8_e4m3fn).astype(np.float64) * np.repeat(np.exp2(scales.astype(np.float64) - 127.0), 8, axis=1)[..., None]
    return vals.transpose(0, 1, 3, 2).reshape(g * 512, n)


def silu(v):
    return v / (1.0 + np.exp(-np.maximum(v, -700.0)))


K, T, H, N = 512, 1024, 512, 256


def setup_inputs():
    n = np.random.standard_normal
    s = mx_kscale(K)[:, None]
    u = mx_kscale(H)
    packed_xT = pack_weight(n((K, T)) * s)
    packed_w3 = pack_weight(n((H, N)) / np.sqrt(H) / u[:, None])
    return {
        "x_words": packed_xT[0],
        "x_scales": packed_xT[1],
        "w1": (n((K, H)) / np.sqrt(2 * K) / s * u).astype(np.float32),
        "w2": (n((K, H)) / np.sqrt(2 * K) / s * u).astype(np.float32),
        "w3_words": packed_w3[0],
        "w3_scales": packed_w3[1],
        "pos1": striped(np.random.permutation(T)),
        "pos2": striped(np.random.permutation(T)),
        "pos3": striped(np.random.permutation(T)),
    }


def reference(x_words, x_scales, w1, w2, w3_words, w3_scales, pos1, pos2, pos3):
    xq = unpack_weight(x_words, x_scales)
    y = mxq(f64(w1), 0, "e4m3").T @ xq
    e = mxq(f64(w2), 0, "e4m3").T @ xq
    z = np.maximum(np.maximum(silu(y + e[:, unstriped(pos1)]), silu(y + e[:, unstriped(pos2)])), silu(y + e[:, unstriped(pos3)]))
    return unpack_weight(w3_words, w3_scales).T @ mxq(z, 0, "e4m3")

@@ -1,0 +1,173 @@
+from contextlib import ExitStack
+
+import concourse.mybir as mybir
+
+K, T, H, N = 512, 1024, 512, 256
+FLOPS = 2 * K * H * T * 2 + 2 * H * N * T
+
+F32 = mybir.dt.float32
+BF16 = mybir.dt.bfloat16
+I32 = mybir.dt.int32
+U32 = mybir.dt.uint32
+U16 = mybir.dt.uint16
+U8 = mybir.dt.uint8
+FP8X4 = mybir.dt.float8_e4m3fn_x4
+ADD = mybir.AluOpType.add
+MAX = mybir.AluOpType.max
+SILU = mybir.ActivationFunctionType.Silu
+
+P = 128
+PACK = 4
+HALF = 512
+CHUNKS = ((0, 512), (512, 256), (768, 256))
+
+
+def load_scale_rows(queue, plane, rows):
+    for q in range(4):
+        queue.dma_start(out=plane[32 * q : 32 * q + 4, :].bitcast(I32), in_=rows[4 * q : 4 * q + 4, :].bitcast(I32))
+
+
+def tile_picked_wedgecv_silu_l_kernel(tc, x_words, x_scales, w1, w2, w3_words, w3_scales, pos1, pos2, pos3, out):
+    nc = tc.nc
+    with ExitStack() as ctx:
+        keep = ctx.enter_context(tc.tile_pool(name="keep", bufs=1))
+        work = ctx.enter_context(tc.tile_pool(name="work", bufs=2))
+        psum = ctx.enter_context(tc.psum_pool(name="psum", bufs=1))
+
+        lists = [keep.tile([P, T // 16], U16, name=f"list{d}") for d in range(3)]
+        x_plane = keep.tile([P, T], U8, align_bytes=64)
+        w3_plane = keep.tile([P, N], U8, align_bytes=64)
+        x_codes = [keep.tile([P, HALF], U32, name=f"x_codes{h}", align_bytes=64) for h in range(2)]
+        w3_codes = keep.tile([P, N], U32, align_bytes=64)
+        w_raw = [keep.tile([P, PACK, H], F32, name=f"w_raw{i}") for i in range(2)]
+        warm = keep.tile([P, 8], F32)
+        warm_out = keep.tile([P, 8], F32)
+
+        nc.vector.memset(x_plane[:].bitcast(I32), 0)
+        nc.vector.memset(w3_plane[:].bitcast(I32), 0)
+        nc.vector.memset(warm[:], 0.0)
+
+        x_rows = x_words[0].rearrange("p n t -> p (n t)")
+        nc.sync.dma_start(out=w_raw[0][:], in_=w2.rearrange("(p j) c -> p j c", j=PACK))
+        load_scale_rows(nc.scalar, x_plane, x_scales[0])
+        nc.scalar.activation(warm_out[:], warm[:], SILU)
+        nc.sync.dma_start(out=w_raw[1][:], in_=w1.rearrange("(p j) c -> p j c", j=PACK))
+        for h in range(2):
+            nc.sync.dma_start(out=x_codes[h][:].bitcast(I32), in_=x_rows[:, 4 * HALF * h : 4 * HALF * (h + 1)].bitcast(I32))
+        for tile, pos in zip(lists, (pos1, pos2, pos3)):
+            nc.sync.dma_start(tile[:], pos)
+        nc.sync.dma_start(out=w3_codes[:].bitcast(I32), in_=w3_words[0].rearrange("p n t -> p (n t)").bitcast(I32))
+        load_scale_rows(nc.sync, w3_plane, w3_scales[0])
+
+        w_codes, w_planes = [], []
+        for i in range(2):
+            grouped = keep.tile([P, PACK, P, PACK], BF16, name=f"grouped{i}", align_bytes=64)
+            nc.vector.tensor_copy(
+                out=grouped[:].rearrange("p t m j -> p m t j"),
+                in_=w_raw[i][:].rearrange("p j (m t) -> p m t j", t=PACK),
+            )
+            codes = keep.tile([P, H], U32, name=f"w_codes{i}", align_bytes=64)
+            plane = keep.tile([P, H], U8, name=f"w_plane{i}", align_bytes=64)
+            for t in range(PACK):
+                cols = slice(P * t, P * (t + 1))
+                nc.vector.quantize_mx(
+                    out=codes[:, cols].bitcast(FP8X4),
+                    scales=plane[:, cols],
+                    in_=grouped[:, t, :, :].rearrange("p m j -> p (m j)"),
+                )
+            w_codes.append(codes)
+            w_planes.append(plane)
+
+        def project(i, t, h, target, engine):
+            acc = psum.tile([P, HALF], F32, name="acc", bufs=6)
+            cols = slice(P * t, P * (t + 1))
+            nc.tensor.matmul_mx(
+                out=acc[:],
+                lhsT=w_codes[i][:, cols].bitcast(FP8X4),
+                lhsT_scale=w_planes[i][:, cols],
+                rhs=x_codes[h][:].bitcast(FP8X4),
+                rhs_scale=x_plane[:, HALF * h : HALF * (h + 1)],
+                start=True,
+                stop=True,
+            )
+            if engine == "vector":
+                nc.vector.tensor_copy(out=target, in_=acc[:])
+            else:
+                nc.scalar.copy(out=target, in_=acc[:])
+
+        e = [keep.tile([P, T], F32, name=f"e{t}") for t in range(PACK)]
+        y = [[keep.tile([P, HALF], F32, name=f"y{t}_{h}") for h in range(2)] for t in range(PACK)]
+
+        def project_first(t):
+            project(0, t, 0, e[t][:, :HALF], "scalar")
+            project(1, t, 0, y[t][0][:], "scalar")
+            project(0, t, 1, e[t][:, HALF:], "vector" if t == 0 else "scalar")
+
+        def edges(c, q, acts):
+            v0, n = CHUNKS[c]
+            h, y0 = divmod(v0, HALF)
+            sums = [work.tile([P, 2, HALF], F32, name="sums", bufs=6) for d in range(3)]
+            for r in range(2):
+                t = 2 * q + r
+                if c == 0:
+                    project_first(t)
+                if c == 1:
+                    project(1, t, 1, y[t][1][:], "scalar")
+                for d in range(3):
+                    nc.vector.tensor_tensor(
+                        sums[d][:, r, :n],
+                        e[t][:].indirect(lists[d][:, v0 // 16 : (v0 + n) // 16]),
+                        y[t][h][:, y0 : y0 + n],
+                        ADD,
+                    )
+                    if r == 1:
+                        nc.scalar.activation(
+                            acts[d][:, q, :n, :], sums[d][:, :, :n].rearrange("p r v -> p v r"), SILU
+                        )
+
+        def finish(c, acts):
+            v0, n = CHUNKS[c]
+            best = work.tile([P, 2, HALF, 2], BF16, name="best")
+            nc.vector.tensor_tensor(best[:, :, :n, :], acts[0][:, :, :n, :], acts[1][:, :, :n, :], MAX)
+            z = work.tile([P, HALF, 2, 2], BF16, name="z", align_bytes=64)
+            nc.vector.tensor_tensor(
+                z[:, :n, :, :],
+                best[:, :, :n, :].rearrange("p q v r -> p v q r"),
+                acts[2][:, :, :n, :].rearrange("p q v r -> p v q r"),
+                MAX,
+            )
+            z_codes = work.tile([P, HALF], U32, name="z_codes", align_bytes=64)
+            z_plane = work.tile([P, HALF], U8, name="z_plane", align_bytes=64)
+            nc.vector.quantize_mx(
+                out=z_codes[:, :n].bitcast(FP8X4),
+                scales=z_plane[:, :n],
+                in_=z[:, :n, :, :].rearrange("p v q r -> p (v q r)"),
+            )
+            for m in range(N // P):
+                cols = slice(P * m, P * (m + 1))
+                acc = psum.tile([P, HALF], F32, name="acc_out", bufs=2)
+                nc.tensor.matmul_mx(
+                    out=acc[:, :n],
+                    lhsT=w3_codes[:, cols].bitcast(FP8X4),
+                    lhsT_scale=w3_plane[:, cols],
+                    rhs=z_codes[:, :n].bitcast(FP8X4),
+                    rhs_scale=z_plane[:, :n],
+                    start=True,
+                    stop=True,
+                )
+                result = work.tile([P, HALF], F32, name="result", bufs=4)
+                if c == len(CHUNKS) - 1 and m == 1:
+                    nc.vector.tensor_copy(out=result[:, :n], in_=acc[:, :n])
+                else:
+                    nc.scalar.copy(out=result[:, :n], in_=acc[:, :n])
+                nc.sync.dma_start(out=out[cols, v0 : v0 + n], in_=result[:, :n])
+
+        previous = None
+        for c in range(len(CHUNKS)):
+            acts = [work.tile([P, 2, HALF, 2], BF16, name=f"acts{d}") for d in range(3)]
+            edges(c, 0, acts)
+            if previous is not None:
+                finish(c - 1, previous)
+            edges(c, 1, acts)
+            previous = acts
+        finish(len(CHUNKS) - 1, previous)

@@ -19,7 +19,10 @@ SILU = mybir.ActivationFunctionType.Silu
 P = 128
 PACK = 4
 HALF = 512
-CHUNKS = ((0, 512), (512, 256), (768, 256))
+SPARE = 16
+HALVES = ((0, 512), (512, 512))
+FIRST_PIECES = ((0, 256), (256, 256), (512, 512))
+CHUNKS = ((0, 256), (256, 256), (512, 256), (768, 128), (896, 128))
 
 
 def load_scale_rows(queue, plane, rows):
@@ -31,7 +34,6 @@ def tile_picked_wedgecv_silu_l_kernel(tc, x_words, x_scales, w1, w2, w3_words, w
     nc = tc.nc
     with ExitStack() as ctx:
         keep = ctx.enter_context(tc.tile_pool(name="keep", bufs=1))
-        work = ctx.enter_context(tc.tile_pool(name="work", bufs=2))
         psum = ctx.enter_context(tc.psum_pool(name="psum", bufs=1))
 
         lists = [keep.tile([P, T // 16], U16, name=f"list{d}") for d in range(3)]
@@ -42,10 +44,14 @@ def tile_picked_wedgecv_silu_l_kernel(tc, x_words, x_scales, w1, w2, w3_words, w
         w_raw = [keep.tile([P, PACK, H], F32, name=f"w_raw{i}") for i in range(2)]
         warm = keep.tile([P, 8], F32)
         warm_out = keep.tile([P, 8], F32)
+        e = [keep.tile([P, T + SPARE], F32, name=f"e{t}") for t in range(PACK)]
+        y = [keep.tile([P, T], F32, name=f"y{t}") for t in range(PACK)]
 
         nc.vector.memset(x_plane[:].bitcast(I32), 0)
-        nc.vector.memset(w3_plane[:].bitcast(I32), 0)
         nc.vector.memset(warm[:], 0.0)
+        nc.vector.memset(w3_plane[:].bitcast(I32), 0)
+        for t in range(PACK):
+            nc.vector.memset(e[t][:, T:], 0.0)
 
         x_rows = x_words[0].rearrange("p n t -> p (n t)")
         nc.sync.dma_start(out=w_raw[0][:], in_=w2.rearrange("(p j) c -> p j c", j=PACK))
@@ -59,115 +65,114 @@ def tile_picked_wedgecv_silu_l_kernel(tc, x_words, x_scales, w1, w2, w3_words, w
         nc.sync.dma_start(out=w3_codes[:].bitcast(I32), in_=w3_words[0].rearrange("p n t -> p (n t)").bitcast(I32))
         load_scale_rows(nc.sync, w3_plane, w3_scales[0])
 
-        w_codes, w_planes = [], []
+        w_codes, w_planes = {}, {}
         for i in range(2):
-            grouped = keep.tile([P, PACK, P, PACK], BF16, name=f"grouped{i}", align_bytes=64)
-            nc.vector.tensor_copy(
-                out=grouped[:].rearrange("p t m j -> p m t j"),
-                in_=w_raw[i][:].rearrange("p j (m t) -> p m t j", t=PACK),
-            )
-            codes = keep.tile([P, H], U32, name=f"w_codes{i}", align_bytes=64)
-            plane = keep.tile([P, H], U8, name=f"w_plane{i}", align_bytes=64)
-            for t in range(PACK):
-                cols = slice(P * t, P * (t + 1))
+            for q in range(2):
+                grouped = keep.tile([P, 2, P, PACK], BF16, name=f"grouped{i}_{q}", align_bytes=64)
+                source = w_raw[i][:].rearrange("p j (m t) -> p m t j", t=PACK)[:, :, 2 * q : 2 * q + 2, :]
+                target = grouped[:].rearrange("p r m j -> p m r j")
+                nc.vector.tensor_copy(out=target, in_=source)
+                codes = keep.tile([P, 2 * P], U32, name=f"w_codes{i}_{q}", align_bytes=64)
+                plane = keep.tile([P, 2 * P], U8, name=f"w_plane{i}_{q}", align_bytes=64)
                 nc.vector.quantize_mx(
-                    out=codes[:, cols].bitcast(FP8X4),
-                    scales=plane[:, cols],
-                    in_=grouped[:, t, :, :].rearrange("p m j -> p (m j)"),
+                    out=codes[:].bitcast(FP8X4), scales=plane[:], in_=grouped[:].rearrange("p r m j -> p (r m j)")
                 )
-            w_codes.append(codes)
-            w_planes.append(plane)
+                w_codes[i, q], w_planes[i, q] = codes, plane
 
-        def project(i, t, h, target, engine):
-            acc = psum.tile([P, HALF], F32, name="acc", bufs=6)
-            cols = slice(P * t, P * (t + 1))
+        def project(i, t, v0, n, target, copy):
+            acc = psum.tile([P, HALF], F32, name="acc", bufs=8)
+            h, c0 = divmod(v0, HALF)
+            q, r = divmod(t, 2)
+            cols = slice(P * r, P * (r + 1))
             nc.tensor.matmul_mx(
-                out=acc[:],
-                lhsT=w_codes[i][:, cols].bitcast(FP8X4),
-                lhsT_scale=w_planes[i][:, cols],
-                rhs=x_codes[h][:].bitcast(FP8X4),
-                rhs_scale=x_plane[:, HALF * h : HALF * (h + 1)],
+                out=acc[:, :n],
+                lhsT=w_codes[i, q][:, cols].bitcast(FP8X4),
+                lhsT_scale=w_planes[i, q][:, cols],
+                rhs=x_codes[h][:, c0 : c0 + n].bitcast(FP8X4),
+                rhs_scale=x_plane[:, v0 : v0 + n],
                 start=True,
                 stop=True,
             )
-            if engine == "vector":
-                nc.vector.tensor_copy(out=target, in_=acc[:])
-            else:
-                nc.scalar.copy(out=target, in_=acc[:])
+            copy(out=target[:, v0 : v0 + n], in_=acc[:, :n])
 
-        e = [keep.tile([P, T], F32, name=f"e{t}") for t in range(PACK)]
-        y = [[keep.tile([P, HALF], F32, name=f"y{t}_{h}") for h in range(2)] for t in range(PACK)]
-
-        def project_first(t):
-            project(0, t, 0, e[t][:, :HALF], "scalar")
-            project(1, t, 0, y[t][0][:], "scalar")
-            project(0, t, 1, e[t][:, HALF:], "vector" if t == 0 else "scalar")
-
-        def edges(c, q, acts):
-            v0, n = CHUNKS[c]
-            h, y0 = divmod(v0, HALF)
-            sums = [work.tile([P, 2, HALF], F32, name="sums", bufs=6) for d in range(3)]
+        acts = [keep.tile([P, 2, T, 2], BF16, name=f"acts{d}") for d in range(3)]
+        for q in range(2):
+            sums = [keep.tile([P, 2, T], F32, name=f"sums{q}_{d}") for d in range(3)]
             for r in range(2):
                 t = 2 * q + r
-                if c == 0:
-                    project_first(t)
-                if c == 1:
-                    project(1, t, 1, y[t][1][:], "scalar")
+                project(0, t, 0, HALF, e[t], nc.scalar.copy)
+                project(0, t, HALF, HALF, e[t], nc.vector.tensor_copy if t == 0 else nc.scalar.copy)
+                for v0, width in FIRST_PIECES if t == 0 else HALVES:
+                    project(1, t, v0, width, y[t], nc.scalar.copy)
                 for d in range(3):
-                    nc.vector.tensor_tensor(
-                        sums[d][:, r, :n],
-                        e[t][:].indirect(lists[d][:, v0 // 16 : (v0 + n) // 16]),
-                        y[t][h][:, y0 : y0 + n],
-                        ADD,
-                    )
-                    if r == 1:
-                        nc.scalar.activation(
-                            acts[d][:, q, :n, :], sums[d][:, :, :n].rearrange("p r v -> p v r"), SILU
+                    for v0, width in FIRST_PIECES if (t, d) == (0, 0) else ((0, T),):
+                        nc.vector.tensor_tensor(
+                            sums[d][:, r, v0 : v0 + width],
+                            e[t][:].indirect(lists[d][:, v0 // 16 : (v0 + width) // 16]),
+                            y[t][:, v0 : v0 + width],
+                            ADD,
                         )
+                    if r == 1:
+                        for v0, width in HALVES if (q, d) == (1, 2) else ((0, T),):
+                            nc.scalar.activation(
+                                acts[d][:, q, v0 : v0 + width, :],
+                                sums[d][:, :, v0 : v0 + width].rearrange("p r v -> p v r"),
+                                SILU,
+                            )
 
-        def finish(c, acts):
+        best = keep.tile([P, 2, T, 2], BF16)
+        z = [keep.tile([P, n, 2, 2], BF16, name=f"z{c}", align_bytes=64) for c, (v0, n) in enumerate(CHUNKS)]
+
+        def max_of_two(v0, n):
+            v = slice(v0, v0 + n)
+            nc.vector.tensor_tensor(best[:, :, v, :], acts[0][:, :, v, :], acts[1][:, :, v, :], MAX)
+
+        def max_of_three(c):
             v0, n = CHUNKS[c]
-            best = work.tile([P, 2, HALF, 2], BF16, name="best")
-            nc.vector.tensor_tensor(best[:, :, :n, :], acts[0][:, :, :n, :], acts[1][:, :, :n, :], MAX)
-            z = work.tile([P, HALF, 2, 2], BF16, name="z", align_bytes=64)
+            v = slice(v0, v0 + n)
             nc.vector.tensor_tensor(
-                z[:, :n, :, :],
-                best[:, :, :n, :].rearrange("p q v r -> p v q r"),
-                acts[2][:, :, :n, :].rearrange("p q v r -> p v q r"),
+                z[c][:],
+                best[:, :, v, :].rearrange("p q v r -> p v q r"),
+                acts[2][:, :, v, :].rearrange("p q v r -> p v q r"),
                 MAX,
             )
-            z_codes = work.tile([P, HALF], U32, name="z_codes", align_bytes=64)
-            z_plane = work.tile([P, HALF], U8, name="z_plane", align_bytes=64)
+
+        def finish(c):
+            v0, n = CHUNKS[c]
+            z_codes = keep.tile([P, n], U32, name=f"z_codes{c}", align_bytes=64)
+            z_plane = keep.tile([P, n], U8, name=f"z_plane{c}", align_bytes=64)
             nc.vector.quantize_mx(
-                out=z_codes[:, :n].bitcast(FP8X4),
-                scales=z_plane[:, :n],
-                in_=z[:, :n, :, :].rearrange("p v q r -> p (v q r)"),
+                out=z_codes[:].bitcast(FP8X4), scales=z_plane[:], in_=z[c][:].rearrange("p v q r -> p (v q r)")
             )
+            acc = psum.tile([P, HALF], F32, name="acc", bufs=8)
             for m in range(N // P):
                 cols = slice(P * m, P * (m + 1))
-                acc = psum.tile([P, HALF], F32, name="acc_out", bufs=2)
                 nc.tensor.matmul_mx(
-                    out=acc[:, :n],
+                    out=acc[:, n * m : n * (m + 1)],
                     lhsT=w3_codes[:, cols].bitcast(FP8X4),
                     lhsT_scale=w3_plane[:, cols],
-                    rhs=z_codes[:, :n].bitcast(FP8X4),
-                    rhs_scale=z_plane[:, :n],
+                    rhs=z_codes[:].bitcast(FP8X4),
+                    rhs_scale=z_plane[:],
                     start=True,
                     stop=True,
                 )
-                result = work.tile([P, HALF], F32, name="result", bufs=4)
-                if c == len(CHUNKS) - 1 and m == 1:
-                    nc.vector.tensor_copy(out=result[:, :n], in_=acc[:, :n])
-                else:
-                    nc.scalar.copy(out=result[:, :n], in_=acc[:, :n])
-                nc.sync.dma_start(out=out[cols, v0 : v0 + n], in_=result[:, :n])
+            result = keep.tile([P, 2 * n], F32, name=f"result{c}")
+            copy = nc.vector.tensor_copy if c == len(CHUNKS) - 1 else nc.scalar.copy
+            copy(out=result[:], in_=acc[:, : 2 * n])
+            nc.sync.dma_start(
+                out=out.rearrange("(m p) v -> p m v", p=P)[:, :, v0 : v0 + n],
+                in_=result[:].rearrange("p (m v) -> p m v", m=2),
+            )
 
-        previous = None
-        for c in range(len(CHUNKS)):
-            acts = [work.tile([P, 2, HALF, 2], BF16, name=f"acts{d}") for d in range(3)]
-            edges(c, 0, acts)
-            if previous is not None:
-                finish(c - 1, previous)
-            edges(c, 1, acts)
-            previous = acts
-        finish(len(CHUNKS) - 1, previous)
+        max_of_two(0, 512)
+        max_of_two(512, 512)
+        max_of_three(0)
+        max_of_three(1)
+        finish(0)
+        finish(1)
+        max_of_three(2)
+        max_of_three(3)
+        finish(2)
+        max_of_three(4)
+        finish(3)
+        finish(4)

@@ -1,6 +1,7 @@
 from contextlib import ExitStack
 
 import concourse.mybir as mybir
+from concourse.masks import make_identity
 
 K, T, H, N = 512, 1024, 512, 256
 FLOPS = 2 * K * H * T * 2 + 2 * H * N * T
@@ -21,7 +22,7 @@ PACK = 4
 HALF = 512
 SPARE = 16
 HALVES = ((0, 512), (512, 512))
-FIRST_PIECES = ((0, 256), (256, 256), (512, 512))
+WHOLE = ((0, 1024),)
 CHUNKS = ((0, 256), (256, 256), (512, 256), (768, 128), (896, 128))
 
 
@@ -57,30 +58,37 @@ def tile_picked_wedgecv_silu_l_kernel(tc, x_words, x_scales, w1, w2, w3_words, w
         nc.sync.dma_start(out=w_raw[0][:], in_=w2.rearrange("(p j) c -> p j c", j=PACK))
         load_scale_rows(nc.scalar, x_plane, x_scales[0])
         nc.scalar.activation(warm_out[:], warm[:], SILU)
-        nc.sync.dma_start(out=w_raw[1][:], in_=w1.rearrange("(p j) c -> p j c", j=PACK))
         for h in range(2):
             nc.sync.dma_start(out=x_codes[h][:].bitcast(I32), in_=x_rows[:, 4 * HALF * h : 4 * HALF * (h + 1)].bitcast(I32))
-        for tile, pos in zip(lists, (pos1, pos2, pos3)):
-            nc.sync.dma_start(tile[:], pos)
+        nc.sync.dma_start(lists[0][:], pos1)
+        nc.sync.dma_start(out=w_raw[1][:], in_=w1.rearrange("(p j) c -> p j c", j=PACK))
+        nc.sync.dma_start(lists[1][:], pos2)
+        nc.sync.dma_start(lists[2][:], pos3)
+        identity = keep.tile([P, P], F32)
+        make_identity(nc, identity[:])
         nc.sync.dma_start(out=w3_codes[:].bitcast(I32), in_=w3_words[0].rearrange("p n t -> p (n t)").bitcast(I32))
         load_scale_rows(nc.sync, w3_plane, w3_scales[0])
 
         w_codes, w_planes = {}, {}
-        for i in range(2):
-            for q in range(2):
-                grouped = keep.tile([P, 2, P, PACK], BF16, name=f"grouped{i}_{q}", align_bytes=64)
-                source = w_raw[i][:].rearrange("p j (m t) -> p m t j", t=PACK)[:, :, 2 * q : 2 * q + 2, :]
-                target = grouped[:].rearrange("p r m j -> p m r j")
-                nc.vector.tensor_copy(out=target, in_=source)
-                codes = keep.tile([P, 2 * P], U32, name=f"w_codes{i}_{q}", align_bytes=64)
-                plane = keep.tile([P, 2 * P], U8, name=f"w_plane{i}_{q}", align_bytes=64)
-                nc.vector.quantize_mx(
-                    out=codes[:].bitcast(FP8X4), scales=plane[:], in_=grouped[:].rearrange("p r m j -> p (r m j)")
-                )
-                w_codes[i, q], w_planes[i, q] = codes, plane
+
+        def quantize_weights(i, q, cast, tag):
+            grouped = keep.tile([P, 2, P, PACK], BF16, name=tag, align_bytes=64)
+            cast(
+                out=grouped[:].rearrange("p r m j -> p m r j"),
+                in_=w_raw[i][:].rearrange("p j (m t) -> p m t j", t=PACK)[:, :, 2 * q : 2 * q + 2, :],
+            )
+            codes = keep.tile([P, 2 * P], U32, name=f"w_codes{i}_{q}", align_bytes=64)
+            plane = keep.tile([P, 2 * P], U8, name=f"w_plane{i}_{q}", align_bytes=64)
+            nc.vector.quantize_mx(
+                out=codes[:].bitcast(FP8X4), scales=plane[:], in_=grouped[:].rearrange("p r m j -> p (r m j)")
+            )
+            w_codes[i, q], w_planes[i, q] = codes, plane
+
+        projected = []
 
         def project(i, t, v0, n, target, copy):
-            acc = psum.tile([P, HALF], F32, name="acc", bufs=8)
+            acc = psum.tile([P, HALF], F32, name=f"bank{len(projected) % 4}")
+            projected.append((i, t, v0))
             h, c0 = divmod(v0, HALF)
             q, r = divmod(t, 2)
             cols = slice(P * r, P * (r + 1))
@@ -96,29 +104,81 @@ def tile_picked_wedgecv_silu_l_kernel(tc, x_words, x_scales, w1, w2, w3_words, w
             copy(out=target[:, v0 : v0 + n], in_=acc[:, :n])
 
         acts = [keep.tile([P, 2, T, 2], BF16, name=f"acts{d}") for d in range(3)]
-        for q in range(2):
-            sums = [keep.tile([P, 2, T], F32, name=f"sums{q}_{d}") for d in range(3)]
-            for r in range(2):
-                t = 2 * q + r
-                project(0, t, 0, HALF, e[t], nc.scalar.copy)
-                project(0, t, HALF, HALF, e[t], nc.vector.tensor_copy if t == 0 else nc.scalar.copy)
-                for v0, width in FIRST_PIECES if t == 0 else HALVES:
-                    project(1, t, v0, width, y[t], nc.scalar.copy)
-                for d in range(3):
-                    for v0, width in FIRST_PIECES if (t, d) == (0, 0) else ((0, T),):
-                        nc.vector.tensor_tensor(
-                            sums[d][:, r, v0 : v0 + width],
-                            e[t][:].indirect(lists[d][:, v0 // 16 : (v0 + width) // 16]),
-                            y[t][:, v0 : v0 + width],
-                            ADD,
-                        )
-                    if r == 1:
-                        for v0, width in HALVES if (q, d) == (1, 2) else ((0, T),):
-                            nc.scalar.activation(
-                                acts[d][:, q, v0 : v0 + width, :],
-                                sums[d][:, :, v0 : v0 + width].rearrange("p r v -> p v r"),
-                                SILU,
-                            )
+
+        def fetch(t, v0, n, tag):
+            picked = keep.tile([P, n], F32, name=tag, align_bytes=64)
+            nc.vector.tensor_copy(picked[:], e[t][:].indirect(lists[0][:, v0 // 16 : (v0 + n) // 16]))
+            return [picked[:, P * b : P * (b + 1)] for b in range(n // P)]
+
+        def fetch_add(t, d, sums, pieces):
+            for v0, n in pieces:
+                nc.vector.tensor_tensor(
+                    sums[:, t % 2, v0 : v0 + n],
+                    e[t][:].indirect(lists[d][:, v0 // 16 : (v0 + n) // 16]),
+                    y[t][:, v0 : v0 + n],
+                    ADD,
+                )
+
+        def activate(q, d, sums, pieces):
+            for v0, n in pieces:
+                nc.scalar.activation(
+                    acts[d][:, q, v0 : v0 + n, :], sums[:, :, v0 : v0 + n].rearrange("p r v -> p v r"), SILU
+                )
+
+        quantize_weights(0, 0, nc.vector.tensor_copy, "grouped00")
+        quantize_weights(0, 1, nc.vector.tensor_copy, "grouped01")
+        project(0, 0, 0, HALF, e[0], nc.scalar.copy)
+        project(0, 0, 512, 256, e[0], nc.vector.tensor_copy)
+        project(0, 0, 768, 256, e[0], nc.vector.tensor_copy)
+        for v0, n in HALVES:
+            project(0, 1, v0, n, e[1], nc.scalar.copy)
+        early = [fetch(0, 0, 768, "early0") + fetch(0, 768, 256, "early1"), fetch(1, 0, 256, "early2")]
+        quantize_weights(1, 0, nc.scalar.copy, "shared")
+        early[1] = early[1] + fetch(1, 256, 768, "shared")
+        for t in range(2):
+            for v0, n in HALVES:
+                project(1, t, v0, n, y[t], nc.scalar.copy)
+        quantize_weights(1, 1, nc.scalar.copy, "grouped11")
+
+        sums = {d: keep.tile([P, 2, T], F32, name=f"sums0_{d}") for d in (1, 2)}
+        fetch_add(0, 1, sums[1], HALVES)
+        fetch_add(0, 2, sums[2], WHOLE)
+        for t in (2, 3):
+            for i, target in ((0, e[t]), (1, y[t])):
+                for v0, n in HALVES:
+                    project(i, t, v0, n, target, nc.scalar.copy)
+        for d in (1, 2):
+            fetch_add(1, d, sums[d], WHOLE)
+            activate(0, d, sums[d], WHOLE)
+
+        turned = keep.tile([P, T // P, P, 2], BF16)
+        for pair in range(T // P // 2):
+            bank = psum.tile([P, 2, 2, P], F32, name=f"bank{4 + pair}")
+            for s in range(2):
+                b = 2 * pair + s
+                for r in range(2):
+                    nc.tensor.matmul(
+                        bank[:, s, r, :], y[r][:, P * b : P * (b + 1)], identity[:], start=True, stop=False, is_transpose=True
+                    )
+                    nc.tensor.matmul(bank[:, s, r, :], early[r][b], identity[:], start=False, stop=True, is_transpose=True)
+            nc.scalar.activation(
+                turned[:, 2 * pair : 2 * pair + 2, :, :], bank[:].rearrange("v s r p -> v s p r"), SILU
+            )
+        turned_words = turned[:].rearrange("v b p r -> v (b p r)").bitcast(F32)
+        for v0, n in HALVES:
+            bank = psum.tile([P, HALF], F32, name=f"bank{4 + v0 // HALF}")
+            for c0 in range(0, n, P):
+                nc.tensor.transpose(bank[:, c0 : c0 + P], turned_words[:, v0 + c0 : v0 + c0 + P], identity[:])
+            nc.scalar.copy(
+                out=acts[0][:, 0, v0 : v0 + n, :].rearrange("p v r -> p (v r)").bitcast(F32), in_=bank[:]
+            )
+
+        sums = [keep.tile([P, 2, T], F32, name=f"sums1_{d}") for d in range(3)]
+        for d in range(3):
+            fetch_add(2, d, sums[d], WHOLE)
+        for d in range(3):
+            fetch_add(3, d, sums[d], WHOLE)
+            activate(1, d, sums[d], HALVES if d == 2 else WHOLE)
 
         best = keep.tile([P, 2, T, 2], BF16)
         z = [keep.tile([P, n, 2, 2], BF16, name=f"z{c}", align_bytes=64) for c, (v0, n) in enumerate(CHUNKS)]
@@ -144,7 +204,7 @@ def tile_picked_wedgecv_silu_l_kernel(tc, x_words, x_scales, w1, w2, w3_words, w
             nc.vector.quantize_mx(
                 out=z_codes[:].bitcast(FP8X4), scales=z_plane[:], in_=z[c][:].rearrange("p v q r -> p (v q r)")
             )
-            acc = psum.tile([P, HALF], F32, name="acc", bufs=8)
+            acc = psum.tile([P, HALF], F32, name=f"bank{c}")
             for m in range(N // P):
                 cols = slice(P * m, P * (m + 1))
                 nc.tensor.matmul_mx(

@@ -48,7 +48,7 @@ def tile_picked_wedgecv_silu_l_kernel(tc, x_words, x_scales, w1, w2, w3_words, w
         e = [keep.tile([P, T + SPARE], F32, name=f"e{t}") for t in range(PACK)]
         y = [keep.tile([P, T], F32, name=f"y{t}") for t in range(PACK)]
 
-        nc.vector.memset(x_plane[:].bitcast(I32), 0)
+        nc.gpsimd.memset(x_plane[:].bitcast(I32), 0)
         nc.vector.memset(warm[:], 0.0)
         nc.vector.memset(w3_plane[:].bitcast(I32), 0)
         for t in range(PACK):
@@ -74,8 +74,8 @@ def tile_picked_wedgecv_silu_l_kernel(tc, x_words, x_scales, w1, w2, w3_words, w
         def quantize_weights(i, q, cast, tag):
             grouped = keep.tile([P, 2, P, PACK], BF16, name=tag, align_bytes=64)
             cast(
-                out=grouped[:].rearrange("p r m j -> p m r j"),
-                in_=w_raw[i][:].rearrange("p j (m t) -> p m t j", t=PACK)[:, :, 2 * q : 2 * q + 2, :],
+                out=grouped[:].rearrange("p r m j -> p m j r"),
+                in_=w_raw[i][:].rearrange("p j (m t) -> p m j t", t=PACK)[:, :, :, 2 * q : 2 * q + 2],
             )
             codes = keep.tile([P, 2 * P], U32, name=f"w_codes{i}_{q}", align_bytes=64)
             plane = keep.tile([P, 2 * P], U8, name=f"w_plane{i}_{q}", align_bytes=64)

@@ -20,15 +20,20 @@ SILU = mybir.ActivationFunctionType.Silu
 P = 128
 PACK = 4
 HALF = 512
+QUARTER = 256
 SPARE = 16
-HALVES = ((0, 512), (512, 512))
-WHOLE = ((0, 1024),)
+PER_COLUMN = 16
+W2, W1 = 0, 1
+PROJECTION_BANKS = 4
+
+WHOLE = ((0, T),)
+HALVES = ((0, HALF), (HALF, HALF))
 CHUNKS = ((0, 256), (256, 256), (512, 256), (768, 128), (896, 128))
 
 
 def load_scale_rows(queue, plane, rows):
-    for q in range(4):
-        queue.dma_start(out=plane[32 * q : 32 * q + 4, :].bitcast(I32), in_=rows[4 * q : 4 * q + 4, :].bitcast(I32))
+    for g in range(4):
+        queue.dma_start(out=plane[32 * g : 32 * g + 4, :].bitcast(I32), in_=rows[4 * g : 4 * g + 4, :].bitcast(I32))
 
 
 def tile_picked_wedgecv_silu_l_kernel(tc, x_words, x_scales, w1, w2, w3_words, w3_scales, pos1, pos2, pos3, out):
@@ -37,31 +42,23 @@ def tile_picked_wedgecv_silu_l_kernel(tc, x_words, x_scales, w1, w2, w3_words, w
         keep = ctx.enter_context(tc.tile_pool(name="keep", bufs=1))
         psum = ctx.enter_context(tc.psum_pool(name="psum", bufs=1))
 
-        lists = [keep.tile([P, T // 16], U16, name=f"list{d}") for d in range(3)]
+        lists = [keep.tile([P, T // PER_COLUMN], U16, name=f"list{d}") for d in range(3)]
         x_plane = keep.tile([P, T], U8, align_bytes=64)
         w3_plane = keep.tile([P, N], U8, align_bytes=64)
         x_codes = [keep.tile([P, HALF], U32, name=f"x_codes{h}", align_bytes=64) for h in range(2)]
         w3_codes = keep.tile([P, N], U32, align_bytes=64)
-        w_raw = [keep.tile([P, PACK, H], F32, name=f"w_raw{i}") for i in range(2)]
-        warm = keep.tile([P, 8], F32)
-        warm_out = keep.tile([P, 8], F32)
+        w_raw = [keep.tile([P, PACK, H], F32, name=f"w_raw{i}") for i in (W2, W1)]
         e = [keep.tile([P, T + SPARE], F32, name=f"e{t}") for t in range(PACK)]
         y = [keep.tile([P, T], F32, name=f"y{t}") for t in range(PACK)]
 
-        nc.gpsimd.memset(x_plane[:].bitcast(I32), 0)
-        nc.vector.memset(warm[:], 0.0)
-        nc.vector.memset(w3_plane[:].bitcast(I32), 0)
-        for t in range(PACK):
-            nc.vector.memset(e[t][:, T:], 0.0)
-
         x_rows = x_words[0].rearrange("p n t -> p (n t)")
-        nc.sync.dma_start(out=w_raw[0][:], in_=w2.rearrange("(p j) c -> p j c", j=PACK))
-        load_scale_rows(nc.scalar, x_plane, x_scales[0])
-        nc.scalar.activation(warm_out[:], warm[:], SILU)
-        for h in range(2):
-            nc.sync.dma_start(out=x_codes[h][:].bitcast(I32), in_=x_rows[:, 4 * HALF * h : 4 * HALF * (h + 1)].bitcast(I32))
         nc.sync.dma_start(lists[0][:], pos1)
-        nc.sync.dma_start(out=w_raw[1][:], in_=w1.rearrange("(p j) c -> p j c", j=PACK))
+        nc.sync.dma_start(out=w_raw[W2][:], in_=w2.rearrange("(p j) c -> p j c", j=PACK))
+        load_scale_rows(nc.scalar, x_plane, x_scales[0])
+        for h in range(2):
+            half_row = x_rows[:, PACK * HALF * h : PACK * HALF * (h + 1)]
+            nc.sync.dma_start(out=x_codes[h][:].bitcast(I32), in_=half_row.bitcast(I32))
+        nc.sync.dma_start(out=w_raw[W1][:], in_=w1.rearrange("(p j) c -> p j c", j=PACK))
         nc.sync.dma_start(lists[1][:], pos2)
         nc.sync.dma_start(lists[2][:], pos3)
         identity = keep.tile([P, P], F32)
@@ -87,7 +84,7 @@ def tile_picked_wedgecv_silu_l_kernel(tc, x_words, x_scales, w1, w2, w3_words, w
         projected = []
 
         def project(i, t, v0, n, target, copy):
-            acc = psum.tile([P, HALF], F32, name=f"bank{len(projected) % 4}")
+            acc = psum.tile([P, HALF], F32, name=f"bank{len(projected) % PROJECTION_BANKS}")
             projected.append((i, t, v0))
             h, c0 = divmod(v0, HALF)
             q, r = divmod(t, 2)
@@ -105,46 +102,48 @@ def tile_picked_wedgecv_silu_l_kernel(tc, x_words, x_scales, w1, w2, w3_words, w
 
         acts = [keep.tile([P, 2, T, 2], BF16, name=f"acts{d}") for d in range(3)]
 
+        def neighbours(t, d, v0, n):
+            return e[t][:].indirect(lists[d][:, v0 // PER_COLUMN : (v0 + n) // PER_COLUMN])
+
         def fetch(t, v0, n, tag):
             picked = keep.tile([P, n], F32, name=tag, align_bytes=64)
-            nc.vector.tensor_copy(picked[:], e[t][:].indirect(lists[0][:, v0 // 16 : (v0 + n) // 16]))
+            nc.vector.tensor_copy(picked[:], neighbours(t, 0, v0, n))
             return [picked[:, P * b : P * (b + 1)] for b in range(n // P)]
 
-        def fetch_add(t, d, sums, pieces):
-            for v0, n in pieces:
+        def fetch_add(t, d, sums, ranges):
+            for v0, n in ranges:
                 nc.vector.tensor_tensor(
-                    sums[:, t % 2, v0 : v0 + n],
-                    e[t][:].indirect(lists[d][:, v0 // 16 : (v0 + n) // 16]),
-                    y[t][:, v0 : v0 + n],
-                    ADD,
+                    sums[:, t % 2, v0 : v0 + n], neighbours(t, d, v0, n), y[t][:, v0 : v0 + n], ADD
                 )
 
-        def activate(q, d, sums, pieces):
-            for v0, n in pieces:
+        def activate(q, d, sums, ranges):
+            for v0, n in ranges:
                 nc.scalar.activation(
                     acts[d][:, q, v0 : v0 + n, :], sums[:, :, v0 : v0 + n].rearrange("p r v -> p v r"), SILU
                 )
 
-        quantize_weights(0, 0, nc.vector.tensor_copy, "grouped00")
-        quantize_weights(0, 1, nc.vector.tensor_copy, "grouped01")
-        project(0, 0, 0, HALF, e[0], nc.scalar.copy)
-        project(0, 0, 512, 256, e[0], nc.vector.tensor_copy)
-        project(0, 0, 768, 256, e[0], nc.vector.tensor_copy)
+        quantize_weights(W2, 0, nc.vector.tensor_copy, "grouped00")
+        quantize_weights(W2, 1, nc.vector.tensor_copy, "grouped01")
+        project(W2, 0, 0, HALF, e[0], nc.scalar.copy)
+        project(W2, 0, HALF, QUARTER, e[0], nc.vector.tensor_copy)
+        project(W2, 0, HALF + QUARTER, QUARTER, e[0], nc.vector.tensor_copy)
         for v0, n in HALVES:
-            project(0, 1, v0, n, e[1], nc.scalar.copy)
-        early = [fetch(0, 0, 768, "early0") + fetch(0, 768, 256, "early1"), fetch(1, 0, 256, "early2")]
-        quantize_weights(1, 0, nc.scalar.copy, "shared")
-        early[1] = early[1] + fetch(1, 256, 768, "shared")
+            project(W2, 1, v0, n, e[1], nc.scalar.copy)
+
+        rest = T - QUARTER
+        early = [fetch(0, 0, rest, "early0") + fetch(0, rest, QUARTER, "early1"), fetch(1, 0, QUARTER, "early2")]
+        quantize_weights(W1, 0, nc.scalar.copy, "shared")
+        early[1] = early[1] + fetch(1, QUARTER, rest, "shared")
         for t in range(2):
             for v0, n in HALVES:
-                project(1, t, v0, n, y[t], nc.scalar.copy)
-        quantize_weights(1, 1, nc.scalar.copy, "grouped11")
+                project(W1, t, v0, n, y[t], nc.scalar.copy)
+        quantize_weights(W1, 1, nc.scalar.copy, "grouped11")
 
         sums = {d: keep.tile([P, 2, T], F32, name=f"sums0_{d}") for d in (1, 2)}
         fetch_add(0, 1, sums[1], HALVES)
         fetch_add(0, 2, sums[2], WHOLE)
         for t in (2, 3):
-            for i, target in ((0, e[t]), (1, y[t])):
+            for i, target in ((W2, e[t]), (W1, y[t])):
                 for v0, n in HALVES:
                     project(i, t, v0, n, target, nc.scalar.copy)
         for d in (1, 2):
@@ -152,26 +151,21 @@ def tile_picked_wedgecv_silu_l_kernel(tc, x_words, x_scales, w1, w2, w3_words, w
             activate(0, d, sums[d], WHOLE)
 
         turned = keep.tile([P, T // P, P, 2], BF16)
-        for pair in range(T // P // 2):
-            bank = psum.tile([P, 2, 2, P], F32, name=f"bank{4 + pair}")
+        for g in range(T // P // 2):
+            bank = psum.tile([P, 2, 2, P], F32, name=f"bank{PROJECTION_BANKS + g}")
             for s in range(2):
-                b = 2 * pair + s
+                b = 2 * g + s
                 for r in range(2):
-                    nc.tensor.matmul(
-                        bank[:, s, r, :], y[r][:, P * b : P * (b + 1)], identity[:], start=True, stop=False, is_transpose=True
-                    )
+                    y_block = y[r][:, P * b : P * (b + 1)]
+                    nc.tensor.matmul(bank[:, s, r, :], y_block, identity[:], start=True, stop=False, is_transpose=True)
                     nc.tensor.matmul(bank[:, s, r, :], early[r][b], identity[:], start=False, stop=True, is_transpose=True)
-            nc.scalar.activation(
-                turned[:, 2 * pair : 2 * pair + 2, :, :], bank[:].rearrange("v s r p -> v s p r"), SILU
-            )
+            nc.scalar.activation(turned[:, 2 * g : 2 * g + 2, :, :], bank[:].rearrange("v s r p -> v s p r"), SILU)
         turned_words = turned[:].rearrange("v b p r -> v (b p r)").bitcast(F32)
         for v0, n in HALVES:
-            bank = psum.tile([P, HALF], F32, name=f"bank{4 + v0 // HALF}")
+            bank = psum.tile([P, HALF], F32, name=f"bank{PROJECTION_BANKS + v0 // HALF}")
             for c0 in range(0, n, P):
                 nc.tensor.transpose(bank[:, c0 : c0 + P], turned_words[:, v0 + c0 : v0 + c0 + P], identity[:])
-            nc.scalar.copy(
-                out=acts[0][:, 0, v0 : v0 + n, :].rearrange("p v r -> p (v r)").bitcast(F32), in_=bank[:]
-            )
+            nc.scalar.copy(out=acts[0][:, 0, v0 : v0 + n, :].rearrange("p v r -> p (v r)").bitcast(F32), in_=bank[:])
 
         sums = [keep.tile([P, 2, T], F32, name=f"sums1_{d}") for d in range(3)]
         for d in range(3):
@@ -224,8 +218,8 @@ def tile_picked_wedgecv_silu_l_kernel(tc, x_words, x_scales, w1, w2, w3_words, w
                 in_=result[:].rearrange("p (m v) -> p m v", m=2),
             )
 
-        max_of_two(0, 512)
-        max_of_two(512, 512)
+        for v0, n in HALVES:
+            max_of_two(v0, n)
         max_of_three(0)
         max_of_three(1)
         finish(0)

@@ -26,7 +26,6 @@ PER_COLUMN = 16
 W2, W1 = 0, 1
 PROJECTION_BANKS = 4
 
-WHOLE = ((0, T),)
 HALVES = ((0, HALF), (HALF, HALF))
 CHUNKS = ((0, 256), (256, 256), (512, 256), (768, 128), (896, 128))
 
@@ -100,7 +99,7 @@ def tile_picked_wedgecv_silu_l_kernel(tc, x_words, x_scales, w1, w2, w3_words, w
             )
             copy(out=target[:, v0 : v0 + n], in_=acc[:, :n])
 
-        acts = [keep.tile([P, 2, T, 2], BF16, name=f"acts{d}") for d in range(3)]
+        acts = [keep.tile([P, 2, T, 2], BF16, name=f"acts{d}", align_bytes=64) for d in range(2)]
 
         def neighbours(t, d, v0, n):
             return e[t][:].indirect(lists[d][:, v0 // PER_COLUMN : (v0 + n) // PER_COLUMN])
@@ -110,17 +109,11 @@ def tile_picked_wedgecv_silu_l_kernel(tc, x_words, x_scales, w1, w2, w3_words, w
             nc.vector.tensor_copy(picked[:], neighbours(t, 0, v0, n))
             return [picked[:, P * b : P * (b + 1)] for b in range(n // P)]
 
-        def fetch_add(t, d, sums, ranges):
-            for v0, n in ranges:
-                nc.vector.tensor_tensor(
-                    sums[:, t % 2, v0 : v0 + n], neighbours(t, d, v0, n), y[t][:, v0 : v0 + n], ADD
-                )
+        def fetch_add(t, d, target, v0, n):
+            nc.vector.tensor_tensor(target, neighbours(t, d, v0, n), y[t][:, v0 : v0 + n], ADD)
 
-        def activate(q, d, sums, ranges):
-            for v0, n in ranges:
-                nc.scalar.activation(
-                    acts[d][:, q, v0 : v0 + n, :], sums[:, :, v0 : v0 + n].rearrange("p r v -> p v r"), SILU
-                )
+        def activate(q, d, sums):
+            nc.scalar.activation(acts[d][:, q, :, :], sums[:].rearrange("p r v -> p v r"), SILU)
 
         quantize_weights(W2, 0, nc.vector.tensor_copy, "grouped00")
         quantize_weights(W2, 1, nc.vector.tensor_copy, "grouped01")
@@ -134,21 +127,24 @@ def tile_picked_wedgecv_silu_l_kernel(tc, x_words, x_scales, w1, w2, w3_words, w
         early = [fetch(0, 0, rest, "early0") + fetch(0, rest, QUARTER, "early1"), fetch(1, 0, QUARTER, "early2")]
         quantize_weights(W1, 0, nc.scalar.copy, "shared")
         early[1] = early[1] + fetch(1, QUARTER, rest, "shared")
+        quantize_weights(W1, 1, nc.scalar.copy, "grouped11")
         for t in range(2):
             for v0, n in HALVES:
                 project(W1, t, v0, n, y[t], nc.scalar.copy)
-        quantize_weights(W1, 1, nc.scalar.copy, "grouped11")
 
-        sums = {d: keep.tile([P, 2, T], F32, name=f"sums0_{d}") for d in (1, 2)}
-        fetch_add(0, 1, sums[1], HALVES)
-        fetch_add(0, 2, sums[2], WHOLE)
+        sums01 = keep.tile([P, 2, T], F32, align_bytes=64)
+        for v0, n in HALVES:
+            fetch_add(0, 1, sums01[:, 0, v0 : v0 + n], v0, n)
+        fetch_add(1, 1, sums01[:, 1, :], 0, T)
         for t in (2, 3):
             for i, target in ((W2, e[t]), (W1, y[t])):
                 for v0, n in HALVES:
                     project(i, t, v0, n, target, nc.scalar.copy)
-        for d in (1, 2):
-            fetch_add(1, d, sums[d], WHOLE)
-            activate(0, d, sums[d], WHOLE)
+
+        sums1 = [keep.tile([P, 2, T], F32, name=f"sums1_{d}") for d in range(2)]
+        for t in (2, 3):
+            for d in range(2):
+                fetch_add(t, d, sums1[d][:, t % 2, :], 0, T)
 
         turned = keep.tile([P, T // P, P, 2], BF16)
         for g in range(T // P // 2):
@@ -160,43 +156,43 @@ def tile_picked_wedgecv_silu_l_kernel(tc, x_words, x_scales, w1, w2, w3_words, w
                     nc.tensor.matmul(bank[:, s, r, :], y_block, identity[:], start=True, stop=False, is_transpose=True)
                     nc.tensor.matmul(bank[:, s, r, :], early[r][b], identity[:], start=False, stop=True, is_transpose=True)
             nc.scalar.activation(turned[:, 2 * g : 2 * g + 2, :, :], bank[:].rearrange("v s r p -> v s p r"), SILU)
+        activate(0, 1, sums01)
         turned_words = turned[:].rearrange("v b p r -> v (b p r)").bitcast(F32)
         for v0, n in HALVES:
             bank = psum.tile([P, HALF], F32, name=f"bank{PROJECTION_BANKS + v0 // HALF}")
             for c0 in range(0, n, P):
                 nc.tensor.transpose(bank[:, c0 : c0 + P], turned_words[:, v0 + c0 : v0 + c0 + P], identity[:])
             nc.scalar.copy(out=acts[0][:, 0, v0 : v0 + n, :].rearrange("p v r -> p (v r)").bitcast(F32), in_=bank[:])
+        for d in range(2):
+            activate(1, d, sums1[d])
 
-        sums = [keep.tile([P, 2, T], F32, name=f"sums1_{d}") for d in range(3)]
-        for d in range(3):
-            fetch_add(2, d, sums[d], WHOLE)
-        for d in range(3):
-            fetch_add(3, d, sums[d], WHOLE)
-            activate(1, d, sums[d], HALVES if d == 2 else WHOLE)
+        last = keep.tile([P, T, PACK], BF16)
 
-        best = keep.tile([P, 2, T, 2], BF16)
-        z = [keep.tile([P, n, 2, 2], BF16, name=f"z{c}", align_bytes=64) for c, (v0, n) in enumerate(CHUNKS)]
+        def third_list(v0, n, tag):
+            sums = keep.tile([P, PACK, n], F32, name=tag, align_bytes=64)
+            for t in range(PACK):
+                fetch_add(t, 2, sums[:, t, :], v0, n)
+            for c0, m in CHUNKS:
+                if v0 <= c0 < v0 + n:
+                    nc.scalar.activation(
+                        last[:, c0 : c0 + m, :], sums[:, :, c0 - v0 : c0 - v0 + m].rearrange("p t v -> p v t"), SILU
+                    )
 
-        def max_of_two(v0, n):
-            v = slice(v0, v0 + n)
-            nc.vector.tensor_tensor(best[:, :, v, :], acts[0][:, :, v, :], acts[1][:, :, v, :], MAX)
+        best_pairs = keep.tile([P, 2, T, 2], BF16)
+        best = keep.tile([P, T, PACK], BF16)
+        z = {}
 
         def max_of_three(c):
             v0, n = CHUNKS[c]
-            v = slice(v0, v0 + n)
-            nc.vector.tensor_tensor(
-                z[c][:],
-                best[:, :, v, :].rearrange("p q v r -> p v q r"),
-                acts[2][:, :, v, :].rearrange("p q v r -> p v q r"),
-                MAX,
-            )
+            z[c] = keep.tile([P, n, PACK], BF16, name=f"z{c}", align_bytes=64)
+            nc.vector.tensor_tensor(z[c][:], best[:, v0 : v0 + n, :], last[:, v0 : v0 + n, :], MAX)
 
         def finish(c):
             v0, n = CHUNKS[c]
             z_codes = keep.tile([P, n], U32, name=f"z_codes{c}", align_bytes=64)
             z_plane = keep.tile([P, n], U8, name=f"z_plane{c}", align_bytes=64)
             nc.vector.quantize_mx(
-                out=z_codes[:].bitcast(FP8X4), scales=z_plane[:], in_=z[c][:].rearrange("p v q r -> p (v q r)")
+                out=z_codes[:].bitcast(FP8X4), scales=z_plane[:], in_=z[c][:].rearrange("p v t -> p (v t)")
             )
             acc = psum.tile([P, HALF], F32, name=f"bank{c}")
             for m in range(N // P):
@@ -218,11 +214,19 @@ def tile_picked_wedgecv_silu_l_kernel(tc, x_words, x_scales, w1, w2, w3_words, w
                 in_=result[:].rearrange("p (m v) -> p m v", m=2),
             )
 
+        third_list(0, HALF, "sums01")
         for v0, n in HALVES:
-            max_of_two(v0, n)
+            v = slice(v0, v0 + n)
+            nc.vector.tensor_tensor(best_pairs[:, :, v, :], acts[0][:, :, v, :], acts[1][:, :, v, :], MAX)
+            nc.scalar.copy(
+                out=best[:, v, :].rearrange("p v t -> p (v t)").bitcast(F32).rearrange("p (v q) -> p v q", q=2),
+                in_=best_pairs[:].rearrange("p q v r -> p q (v r)").bitcast(F32)[:, :, v].rearrange("p q v -> p v q"),
+            )
+        third_list(HALF, QUARTER, "acts1")
         max_of_three(0)
         max_of_three(1)
         finish(0)
+        third_list(HALF + QUARTER, QUARTER, "z0")
         finish(1)
         max_of_three(2)
         max_of_three(3)

@@ -21,12 +21,14 @@ P = 128
 PACK = 4
 HALF = 512
 QUARTER = 256
+SPARE_PLAIN = 352
 SPARE = 16
 PER_COLUMN = 16
 W2, W1 = 0, 1
 PROJECTION_BANKS = 4
 
 HALVES = ((0, HALF), (HALF, HALF))
+SPANS = ((0, 512), (512, 256), (768, 256))
 CHUNKS = ((0, 256), (256, 256), (512, 256), (768, 128), (896, 128))
 
 
@@ -47,7 +49,7 @@ def tile_picked_wedgecv_silu_l_kernel(tc, x_words, x_scales, w1, w2, w3_words, w
         x_codes = [keep.tile([P, HALF], U32, name=f"x_codes{h}", align_bytes=64) for h in range(2)]
         w3_codes = keep.tile([P, N], U32, align_bytes=64)
         w_raw = [keep.tile([P, PACK, H], F32, name=f"w_raw{i}") for i in (W2, W1)]
-        e = [keep.tile([P, T + SPARE], F32, name=f"e{t}") for t in range(PACK)]
+        e = [keep.tile([P, T + (SPARE_PLAIN if t < 2 else SPARE)], F32, name=f"e{t}") for t in range(PACK)]
         y = [keep.tile([P, T], F32, name=f"y{t}") for t in range(PACK)]
 
         x_rows = x_words[0].rearrange("p n t -> p (n t)")
@@ -67,31 +69,32 @@ def tile_picked_wedgecv_silu_l_kernel(tc, x_words, x_scales, w1, w2, w3_words, w
 
         w_codes, w_planes = {}, {}
 
-        def quantize_weights(i, q, cast, tag):
-            grouped = keep.tile([P, 2, P, PACK], BF16, name=tag, align_bytes=64)
+        def quantize_weights(i, t0, count, cast, tag):
+            grouped = keep.tile([P, count, P, PACK], BF16, name=tag, align_bytes=64)
             cast(
                 out=grouped[:].rearrange("p r m j -> p m j r"),
-                in_=w_raw[i][:].rearrange("p j (m t) -> p m j t", t=PACK)[:, :, :, 2 * q : 2 * q + 2],
+                in_=w_raw[i][:].rearrange("p j (m t) -> p m j t", t=PACK)[:, :, :, t0 : t0 + count],
             )
-            codes = keep.tile([P, 2 * P], U32, name=f"w_codes{i}_{q}", align_bytes=64)
-            plane = keep.tile([P, 2 * P], U8, name=f"w_plane{i}_{q}", align_bytes=64)
+            codes = keep.tile([P, count * P], U32, name=f"w_codes{i}_{t0}", align_bytes=64)
+            plane = keep.tile([P, count * P], U8, name=f"w_plane{i}_{t0}", align_bytes=64)
             nc.vector.quantize_mx(
                 out=codes[:].bitcast(FP8X4), scales=plane[:], in_=grouped[:].rearrange("p r m j -> p (r m j)")
             )
-            w_codes[i, q], w_planes[i, q] = codes, plane
+            for r in range(count):
+                w_codes[i, t0 + r], w_planes[i, t0 + r] = codes[:, P * r : P * (r + 1)], plane[:, P * r : P * (r + 1)]
 
         projected = []
 
-        def project(i, t, v0, n, target, copy):
-            acc = psum.tile([P, HALF], F32, name=f"bank{len(projected) % PROJECTION_BANKS}")
-            projected.append((i, t, v0))
+        def project(i, t, v0, n, target, copy, bank=None):
+            if bank is None:
+                bank = len(projected) % PROJECTION_BANKS
+                projected.append((i, t, v0))
+            acc = psum.tile([P, HALF], F32, name=f"bank{bank}")
             h, c0 = divmod(v0, HALF)
-            q, r = divmod(t, 2)
-            cols = slice(P * r, P * (r + 1))
             nc.tensor.matmul_mx(
                 out=acc[:, :n],
-                lhsT=w_codes[i, q][:, cols].bitcast(FP8X4),
-                lhsT_scale=w_planes[i, q][:, cols],
+                lhsT=w_codes[i, t].bitcast(FP8X4),
+                lhsT_scale=w_planes[i, t],
                 rhs=x_codes[h][:, c0 : c0 + n].bitcast(FP8X4),
                 rhs_scale=x_plane[:, v0 : v0 + n],
                 start=True,
@@ -100,6 +103,7 @@ def tile_picked_wedgecv_silu_l_kernel(tc, x_words, x_scales, w1, w2, w3_words, w
             copy(out=target[:, v0 : v0 + n], in_=acc[:, :n])
 
         acts = [keep.tile([P, 2, T, 2], BF16, name=f"acts{d}", align_bytes=64) for d in range(2)]
+        last = [keep.tile([P, 2, QUARTER, 2], BF16, name=f"last{k}", align_bytes=64) for k in range(T // QUARTER)]
 
         def neighbours(t, d, v0, n):
             return e[t][:].indirect(lists[d][:, v0 // PER_COLUMN : (v0 + n) // PER_COLUMN])
@@ -112,39 +116,41 @@ def tile_picked_wedgecv_silu_l_kernel(tc, x_words, x_scales, w1, w2, w3_words, w
         def fetch_add(t, d, target, v0, n):
             nc.vector.tensor_tensor(target, neighbours(t, d, v0, n), y[t][:, v0 : v0 + n], ADD)
 
-        def activate(q, d, sums):
-            nc.scalar.activation(acts[d][:, q, :, :], sums[:].rearrange("p r v -> p v r"), SILU)
+        def activate(q, d, sums, v0, n):
+            target = acts[d][:, q] if d < 2 else last[v0 // QUARTER][:, q]
+            nc.scalar.activation(target, sums[:, :, v0 : v0 + n].rearrange("p r v -> p v r"), SILU)
 
-        quantize_weights(W2, 0, nc.vector.tensor_copy, "grouped00")
-        quantize_weights(W2, 1, nc.vector.tensor_copy, "grouped01")
+        quantize_weights(W2, 0, 2, nc.vector.tensor_copy, "grouped00")
+        quantize_weights(W2, 2, 2, nc.vector.tensor_copy, "grouped02")
         project(W2, 0, 0, HALF, e[0], nc.scalar.copy)
         project(W2, 0, HALF, QUARTER, e[0], nc.vector.tensor_copy)
         project(W2, 0, HALF + QUARTER, QUARTER, e[0], nc.vector.tensor_copy)
         for v0, n in HALVES:
             project(W2, 1, v0, n, e[1], nc.scalar.copy)
 
-        rest = T - QUARTER
-        early = [fetch(0, 0, rest, "early0") + fetch(0, rest, QUARTER, "early1"), fetch(1, 0, QUARTER, "early2")]
-        quantize_weights(W1, 0, nc.scalar.copy, "shared")
-        early[1] = early[1] + fetch(1, QUARTER, rest, "shared")
-        quantize_weights(W1, 1, nc.scalar.copy, "grouped11")
-        for t in range(2):
-            for v0, n in HALVES:
-                project(W1, t, v0, n, y[t], nc.scalar.copy)
-
-        sums01 = keep.tile([P, 2, T], F32, align_bytes=64)
+        early = [fetch(0, 0, T, "early0")]
+        quantize_weights(W1, 0, 2, nc.scalar.copy, "shared")
+        early.append(fetch(1, 0, T, "shared"))
         for v0, n in HALVES:
-            fetch_add(0, 1, sums01[:, 0, v0 : v0 + n], v0, n)
-        fetch_add(1, 1, sums01[:, 1, :], 0, T)
-        for t in (2, 3):
-            for i, target in ((W2, e[t]), (W1, y[t])):
-                for v0, n in HALVES:
-                    project(i, t, v0, n, target, nc.scalar.copy)
+            project(W1, 0, v0, n, y[0], nc.scalar.copy)
+        for v0, n in HALVES:
+            project(W1, 1, v0, n, y[1], nc.scalar.copy)
+        quantize_weights(W1, 2, 2, nc.scalar.copy, f"w_codes{W1}_0")
+        for i, target in ((W2, e), (W1, y)):
+            for v0, n in HALVES:
+                for t in (2, 3):
+                    project(i, t, v0, n, target[t], nc.scalar.copy)
 
-        sums1 = [keep.tile([P, 2, T], F32, name=f"sums1_{d}") for d in range(2)]
-        for t in (2, 3):
-            for d in range(2):
-                fetch_add(t, d, sums1[d][:, t % 2, :], 0, T)
+        sums = {}
+        for q, d in ((0, 1), (0, 2), (1, 0), (1, 1), (1, 2)):
+            tag = f"w_codes{W1}_0" if (q, d) == (0, 2) else f"sums{q}_{d}"
+            sums[q, d] = keep.tile([P, 2, T], F32, name=tag, align_bytes=64)
+        for d in (1, 2):
+            for t in range(2):
+                fetch_add(t, d, sums[0, d][:, t, :], 0, T)
+        for d in range(3):
+            for r in range(2):
+                fetch_add(2 + r, d, sums[1, d][:, r, :], 0, T)
 
         turned = keep.tile([P, T // P, P, 2], BF16)
         for g in range(T // P // 2):
@@ -156,43 +162,43 @@ def tile_picked_wedgecv_silu_l_kernel(tc, x_words, x_scales, w1, w2, w3_words, w
                     nc.tensor.matmul(bank[:, s, r, :], y_block, identity[:], start=True, stop=False, is_transpose=True)
                     nc.tensor.matmul(bank[:, s, r, :], early[r][b], identity[:], start=False, stop=True, is_transpose=True)
             nc.scalar.activation(turned[:, 2 * g : 2 * g + 2, :, :], bank[:].rearrange("v s r p -> v s p r"), SILU)
-        activate(0, 1, sums01)
         turned_words = turned[:].rearrange("v b p r -> v (b p r)").bitcast(F32)
         for v0, n in HALVES:
             bank = psum.tile([P, HALF], F32, name=f"bank{PROJECTION_BANKS + v0 // HALF}")
             for c0 in range(0, n, P):
                 nc.tensor.transpose(bank[:, c0 : c0 + P], turned_words[:, v0 + c0 : v0 + c0 + P], identity[:])
             nc.scalar.copy(out=acts[0][:, 0, v0 : v0 + n, :].rearrange("p v r -> p (v r)").bitcast(F32), in_=bank[:])
-        for d in range(2):
-            activate(1, d, sums1[d])
+        for q, d in ((0, 1), (0, 2), (1, 0), (1, 1), (1, 2)):
+            n = T if d < 2 else QUARTER
+            for v0 in range(0, T, n):
+                activate(q, d, sums[q, d], v0, n)
 
-        last = keep.tile([P, T, PACK], BF16)
+        best, z = {}, {}
 
-        def third_list(v0, n, tag):
-            sums = keep.tile([P, PACK, n], F32, name=tag, align_bytes=64)
-            for t in range(PACK):
-                fetch_add(t, 2, sums[:, t, :], v0, n)
-            for c0, m in CHUNKS:
-                if v0 <= c0 < v0 + n:
-                    nc.scalar.activation(
-                        last[:, c0 : c0 + m, :], sums[:, :, c0 - v0 : c0 - v0 + m].rearrange("p t v -> p v t"), SILU
-                    )
-
-        best_pairs = keep.tile([P, 2, T, 2], BF16)
-        best = keep.tile([P, T, PACK], BF16)
-        z = {}
+        def max_of_two(h):
+            v0, n = SPANS[h]
+            v = slice(v0, v0 + n)
+            best[h] = keep.tile([P, 2, n, 2], BF16, name=f"best{h}", align_bytes=64)
+            nc.vector.tensor_tensor(best[h][:], acts[0][:, :, v, :], acts[1][:, :, v, :], MAX)
 
         def max_of_three(c):
             v0, n = CHUNKS[c]
-            z[c] = keep.tile([P, n, PACK], BF16, name=f"z{c}", align_bytes=64)
-            nc.vector.tensor_tensor(z[c][:], best[:, v0 : v0 + n, :], last[:, v0 : v0 + n, :], MAX)
+            h = max(k for k in range(len(SPANS)) if SPANS[k][0] <= v0)
+            c0 = v0 - SPANS[h][0]
+            z[c] = keep.tile([P, n, 2, 2], BF16, name=f"z{c}", align_bytes=64)
+            nc.vector.tensor_tensor(
+                z[c][:],
+                best[h][:, :, c0 : c0 + n, :].rearrange("p q v r -> p v q r"),
+                last[v0 // QUARTER][:, :, v0 % QUARTER : v0 % QUARTER + n, :].rearrange("p q v r -> p v q r"),
+                MAX,
+            )
 
         def finish(c):
             v0, n = CHUNKS[c]
             z_codes = keep.tile([P, n], U32, name=f"z_codes{c}", align_bytes=64)
             z_plane = keep.tile([P, n], U8, name=f"z_plane{c}", align_bytes=64)
             nc.vector.quantize_mx(
-                out=z_codes[:].bitcast(FP8X4), scales=z_plane[:], in_=z[c][:].rearrange("p v t -> p (v t)")
+                out=z_codes[:].bitcast(FP8X4), scales=z_plane[:], in_=z[c][:].rearrange("p v q r -> p (v q r)")
             )
             acc = psum.tile([P, HALF], F32, name=f"bank{c}")
             for m in range(N // P):
@@ -214,23 +220,16 @@ def tile_picked_wedgecv_silu_l_kernel(tc, x_words, x_scales, w1, w2, w3_words, w
                 in_=result[:].rearrange("p (m v) -> p m v", m=2),
             )
 
-        third_list(0, HALF, "sums01")
-        for v0, n in HALVES:
-            v = slice(v0, v0 + n)
-            nc.vector.tensor_tensor(best_pairs[:, :, v, :], acts[0][:, :, v, :], acts[1][:, :, v, :], MAX)
-            nc.scalar.copy(
-                out=best[:, v, :].rearrange("p v t -> p (v t)").bitcast(F32).rearrange("p (v q) -> p v q", q=2),
-                in_=best_pairs[:].rearrange("p q v r -> p q (v r)").bitcast(F32)[:, :, v].rearrange("p q v -> p v q"),
-            )
-        third_list(HALF, QUARTER, "acts1")
+        max_of_two(0)
+        max_of_two(1)
         max_of_three(0)
         max_of_three(1)
         finish(0)
-        third_list(HALF + QUARTER, QUARTER, "z0")
-        finish(1)
         max_of_three(2)
-        max_of_three(3)
+        finish(1)
+        max_of_two(2)
         finish(2)
+        max_of_three(3)
         max_of_three(4)
         finish(3)
         finish(4)

@@ -131,11 +131,11 @@ def tile_picked_wedgecv_silu_l_kernel(tc, x_words, x_scales, w1, w2, w3_words, w
         early = [fetch(0, 0, T, "early0")]
         quantize_weights(W1, 0, 2, nc.scalar.copy, "shared")
         early.append(fetch(1, 0, T, "shared"))
+        quantize_weights(W1, 2, 2, nc.scalar.copy, "sums0_1")
         for v0, n in HALVES:
             project(W1, 0, v0, n, y[0], nc.scalar.copy)
         for v0, n in HALVES:
             project(W1, 1, v0, n, y[1], nc.scalar.copy)
-        quantize_weights(W1, 2, 2, nc.scalar.copy, f"w_codes{W1}_0")
         for i, target in ((W2, e), (W1, y)):
             for v0, n in HALVES:
                 for t in (2, 3):
@@ -143,8 +143,7 @@ def tile_picked_wedgecv_silu_l_kernel(tc, x_words, x_scales, w1, w2, w3_words, w
 
         sums = {}
         for q, d in ((0, 1), (0, 2), (1, 0), (1, 1), (1, 2)):
-            tag = f"w_codes{W1}_0" if (q, d) == (0, 2) else f"sums{q}_{d}"
-            sums[q, d] = keep.tile([P, 2, T], F32, name=tag, align_bytes=64)
+            sums[q, d] = keep.tile([P, 2, T], F32, name=f"sums{q}_{d}", align_bytes=64)
         for d in (1, 2):
             for t in range(2):
                 fetch_add(t, d, sums[0, d][:, t, :], 0, T)

@@ -21,14 +21,14 @@ P = 128
 PACK = 4
 HALF = 512
 QUARTER = 256
-SPARE_PLAIN = 352
 SPARE = 16
+SPARE_PLAIN = 352
 PER_COLUMN = 16
 W2, W1 = 0, 1
 PROJECTION_BANKS = 4
 
 HALVES = ((0, HALF), (HALF, HALF))
-SPANS = ((0, 512), (512, 256), (768, 256))
+SPANS = ((0, 512), (512, 256), (768, 128), (896, 128))
 CHUNKS = ((0, 256), (256, 256), (512, 256), (768, 128), (896, 128))
 
 
@@ -69,27 +69,26 @@ def tile_picked_wedgecv_silu_l_kernel(tc, x_words, x_scales, w1, w2, w3_words, w
 
         w_codes, w_planes = {}, {}
 
-        def quantize_weights(i, t0, count, cast, tag):
-            grouped = keep.tile([P, count, P, PACK], BF16, name=tag, align_bytes=64)
+        def quantize_weights(i, q, cast, tag):
+            grouped = keep.tile([P, 2, P, PACK], BF16, name=tag, align_bytes=64)
             cast(
                 out=grouped[:].rearrange("p r m j -> p m j r"),
-                in_=w_raw[i][:].rearrange("p j (m t) -> p m j t", t=PACK)[:, :, :, t0 : t0 + count],
+                in_=w_raw[i][:].rearrange("p j (m t) -> p m j t", t=PACK)[:, :, :, 2 * q : 2 * q + 2],
             )
-            codes = keep.tile([P, count * P], U32, name=f"w_codes{i}_{t0}", align_bytes=64)
-            plane = keep.tile([P, count * P], U8, name=f"w_plane{i}_{t0}", align_bytes=64)
+            codes = keep.tile([P, 2 * P], U32, name=f"w_codes{i}_{q}", align_bytes=64)
+            plane = keep.tile([P, 2 * P], U8, name=f"w_plane{i}_{q}", align_bytes=64)
             nc.vector.quantize_mx(
                 out=codes[:].bitcast(FP8X4), scales=plane[:], in_=grouped[:].rearrange("p r m j -> p (r m j)")
             )
-            for r in range(count):
-                w_codes[i, t0 + r], w_planes[i, t0 + r] = codes[:, P * r : P * (r + 1)], plane[:, P * r : P * (r + 1)]
+            for r in range(2):
+                cols = slice(P * r, P * (r + 1))
+                w_codes[i, 2 * q + r], w_planes[i, 2 * q + r] = codes[:, cols], plane[:, cols]
 
         projected = []
 
-        def project(i, t, v0, n, target, copy, bank=None):
-            if bank is None:
-                bank = len(projected) % PROJECTION_BANKS
-                projected.append((i, t, v0))
-            acc = psum.tile([P, HALF], F32, name=f"bank{bank}")
+        def project(i, t, v0, n, target, copy):
+            acc = psum.tile([P, HALF], F32, name=f"bank{len(projected) % PROJECTION_BANKS}")
+            projected.append((i, t, v0))
             h, c0 = divmod(v0, HALF)
             nc.tensor.matmul_mx(
                 out=acc[:, :n],
@@ -113,43 +112,45 @@ def tile_picked_wedgecv_silu_l_kernel(tc, x_words, x_scales, w1, w2, w3_words, w
             nc.vector.tensor_copy(picked[:], neighbours(t, 0, v0, n))
             return [picked[:, P * b : P * (b + 1)] for b in range(n // P)]
 
-        def fetch_add(t, d, target, v0, n):
+        sums = {}
+
+        def fetch_add(t, d, v0, n):
+            target = sums[t // 2, d][:, t % 2, v0 : v0 + n]
             nc.vector.tensor_tensor(target, neighbours(t, d, v0, n), y[t][:, v0 : v0 + n], ADD)
 
-        def activate(q, d, sums, v0, n):
+        def activate(q, d, v0, n):
             target = acts[d][:, q] if d < 2 else last[v0 // QUARTER][:, q]
-            nc.scalar.activation(target, sums[:, :, v0 : v0 + n].rearrange("p r v -> p v r"), SILU)
+            nc.scalar.activation(target, sums[q, d][:, :, v0 : v0 + n].rearrange("p r v -> p v r"), SILU)
 
-        quantize_weights(W2, 0, 2, nc.vector.tensor_copy, "grouped00")
-        quantize_weights(W2, 2, 2, nc.vector.tensor_copy, "grouped02")
+        quantize_weights(W2, 0, nc.vector.tensor_copy, "grouped0")
+        quantize_weights(W2, 1, nc.vector.tensor_copy, "grouped1")
         project(W2, 0, 0, HALF, e[0], nc.scalar.copy)
         project(W2, 0, HALF, QUARTER, e[0], nc.vector.tensor_copy)
         project(W2, 0, HALF + QUARTER, QUARTER, e[0], nc.vector.tensor_copy)
         for v0, n in HALVES:
             project(W2, 1, v0, n, e[1], nc.scalar.copy)
 
-        early = [fetch(0, 0, T, "early0")]
-        quantize_weights(W1, 0, 2, nc.scalar.copy, "shared")
-        early.append(fetch(1, 0, T, "shared"))
-        quantize_weights(W1, 2, 2, nc.scalar.copy, "sums0_1")
-        for v0, n in HALVES:
-            project(W1, 0, v0, n, y[0], nc.scalar.copy)
-        for v0, n in HALVES:
-            project(W1, 1, v0, n, y[1], nc.scalar.copy)
+        early = [fetch(0, 0, T, "early0"), fetch(1, 0, QUARTER, "early1")]
+        quantize_weights(W1, 0, nc.scalar.copy, "shared")
+        early[1] = early[1] + fetch(1, QUARTER, T - QUARTER, "shared")
+        quantize_weights(W1, 1, nc.scalar.copy, "sums0_2")
+        for t in range(2):
+            for v0, n in HALVES:
+                project(W1, t, v0, n, y[t], nc.scalar.copy)
         for i, target in ((W2, e), (W1, y)):
             for v0, n in HALVES:
                 for t in (2, 3):
                     project(i, t, v0, n, target[t], nc.scalar.copy)
 
-        sums = {}
         for q, d in ((0, 1), (0, 2), (1, 0), (1, 1), (1, 2)):
             sums[q, d] = keep.tile([P, 2, T], F32, name=f"sums{q}_{d}", align_bytes=64)
-        for d in (1, 2):
-            for t in range(2):
-                fetch_add(t, d, sums[0, d][:, t, :], 0, T)
+        for t in range(2):
+            for d in (1, 2):
+                for v0, n in HALVES if (t, d) == (0, 1) else ((0, T),):
+                    fetch_add(t, d, v0, n)
         for d in range(3):
-            for r in range(2):
-                fetch_add(2 + r, d, sums[1, d][:, r, :], 0, T)
+            for t in (2, 3):
+                fetch_add(t, d, 0, T)
 
         turned = keep.tile([P, T // P, P, 2], BF16)
         for g in range(T // P // 2):
@@ -167,27 +168,27 @@ def tile_picked_wedgecv_silu_l_kernel(tc, x_words, x_scales, w1, w2, w3_words, w
             for c0 in range(0, n, P):
                 nc.tensor.transpose(bank[:, c0 : c0 + P], turned_words[:, v0 + c0 : v0 + c0 + P], identity[:])
             nc.scalar.copy(out=acts[0][:, 0, v0 : v0 + n, :].rearrange("p v r -> p (v r)").bitcast(F32), in_=bank[:])
-        for q, d in ((0, 1), (0, 2), (1, 0), (1, 1), (1, 2)):
+        for q, d in sums:
             n = T if d < 2 else QUARTER
             for v0 in range(0, T, n):
-                activate(q, d, sums[q, d], v0, n)
+                activate(q, d, v0, n)
 
         best, z = {}, {}
 
-        def max_of_two(h):
-            v0, n = SPANS[h]
+        def max_of_two(span):
+            v0, n = SPANS[span]
             v = slice(v0, v0 + n)
-            best[h] = keep.tile([P, 2, n, 2], BF16, name=f"best{h}", align_bytes=64)
-            nc.vector.tensor_tensor(best[h][:], acts[0][:, :, v, :], acts[1][:, :, v, :], MAX)
+            best[span] = keep.tile([P, 2, n, 2], BF16, name=f"best{span}", align_bytes=64)
+            nc.vector.tensor_tensor(best[span][:], acts[0][:, :, v, :], acts[1][:, :, v, :], MAX)
 
         def max_of_three(c):
             v0, n = CHUNKS[c]
-            h = max(k for k in range(len(SPANS)) if SPANS[k][0] <= v0)
-            c0 = v0 - SPANS[h][0]
+            span = max(k for k in range(len(SPANS)) if SPANS[k][0] <= v0)
+            c0 = v0 - SPANS[span][0]
             z[c] = keep.tile([P, n, 2, 2], BF16, name=f"z{c}", align_bytes=64)
             nc.vector.tensor_tensor(
                 z[c][:],
-                best[h][:, :, c0 : c0 + n, :].rearrange("p q v r -> p v q r"),
+                best[span][:, :, c0 : c0 + n, :].rearrange("p q v r -> p v q r"),
                 last[v0 // QUARTER][:, :, v0 % QUARTER : v0 % QUARTER + n, :].rearrange("p q v r -> p v q r"),
                 MAX,
             )
@@ -229,6 +230,7 @@ def tile_picked_wedgecv_silu_l_kernel(tc, x_words, x_scales, w1, w2, w3_words, w
         max_of_two(2)
         finish(2)
         max_of_three(3)
-        max_of_three(4)
+        max_of_two(3)
         finish(3)
+        max_of_three(4)
         finish(4)

@@ -16,6 +16,7 @@ FP8X4 = mybir.dt.float8_e4m3fn_x4
 ADD = mybir.AluOpType.add
 MAX = mybir.AluOpType.max
 SILU = mybir.ActivationFunctionType.Silu
+COPY = mybir.ActivationFunctionType.Copy
 
 P = 128
 PACK = 4
@@ -28,7 +29,7 @@ W2, W1 = 0, 1
 PROJECTION_BANKS = 4
 
 HALVES = ((0, HALF), (HALF, HALF))
-SPANS = ((0, 512), (512, 256), (768, 128), (896, 128))
+SPANS = ((0, 256), (256, 256), (512, 256), (768, 128), (896, 128))
 CHUNKS = ((0, 256), (256, 256), (512, 256), (768, 128), (896, 128))
 
 
@@ -49,7 +50,7 @@ def tile_picked_wedgecv_silu_l_kernel(tc, x_words, x_scales, w1, w2, w3_words, w
         x_codes = [keep.tile([P, HALF], U32, name=f"x_codes{h}", align_bytes=64) for h in range(2)]
         w3_codes = keep.tile([P, N], U32, align_bytes=64)
         w_raw = [keep.tile([P, PACK, H], F32, name=f"w_raw{i}") for i in (W2, W1)]
-        e = [keep.tile([P, T + (SPARE_PLAIN if t < 2 else SPARE)], F32, name=f"e{t}") for t in range(PACK)]
+        e = [keep.tile([P, T + (SPARE_PLAIN if t == 0 else SPARE)], F32, name=f"e{t}") for t in range(PACK)]
         y = [keep.tile([P, T], F32, name=f"y{t}") for t in range(PACK)]
 
         x_rows = x_words[0].rearrange("p n t -> p (n t)")
@@ -86,9 +87,11 @@ def tile_picked_wedgecv_silu_l_kernel(tc, x_words, x_scales, w1, w2, w3_words, w
 
         projected = []
 
-        def project(i, t, v0, n, target, copy):
-            acc = psum.tile([P, HALF], F32, name=f"bank{len(projected) % PROJECTION_BANKS}")
-            projected.append((i, t, v0))
+        def project(i, t, v0, n, target, copy, bank=None):
+            if bank is None:
+                bank = len(projected) % PROJECTION_BANKS
+                projected.append((i, t, v0))
+            acc = psum.tile([P, HALF], F32, name=f"bank{bank}")
             h, c0 = divmod(v0, HALF)
             nc.tensor.matmul_mx(
                 out=acc[:, :n],
@@ -101,15 +104,18 @@ def tile_picked_wedgecv_silu_l_kernel(tc, x_words, x_scales, w1, w2, w3_words, w
             )
             copy(out=target[:, v0 : v0 + n], in_=acc[:, :n])
 
-        acts = [keep.tile([P, 2, T, 2], BF16, name=f"acts{d}", align_bytes=64) for d in range(2)]
+        acts = keep.tile([P, 2, T, 2], BF16, align_bytes=64)
         last = [keep.tile([P, 2, QUARTER, 2], BF16, name=f"last{k}", align_bytes=64) for k in range(T // QUARTER)]
 
         def neighbours(t, d, v0, n):
             return e[t][:].indirect(lists[d][:, v0 // PER_COLUMN : (v0 + n) // PER_COLUMN])
 
-        def fetch(t, v0, n, tag):
+        def fetch(t, v0, n, tag, on_scalar):
             picked = keep.tile([P, n], F32, name=tag, align_bytes=64)
-            nc.vector.tensor_copy(picked[:], neighbours(t, 0, v0, n))
+            if on_scalar:
+                nc.scalar.activation(picked[:], neighbours(t, 0, v0, n), COPY)
+            else:
+                nc.vector.tensor_copy(picked[:], neighbours(t, 0, v0, n))
             return [picked[:, P * b : P * (b + 1)] for b in range(n // P)]
 
         sums = {}
@@ -119,7 +125,7 @@ def tile_picked_wedgecv_silu_l_kernel(tc, x_words, x_scales, w1, w2, w3_words, w
             nc.vector.tensor_tensor(target, neighbours(t, d, v0, n), y[t][:, v0 : v0 + n], ADD)
 
         def activate(q, d, v0, n):
-            target = acts[d][:, q] if d < 2 else last[v0 // QUARTER][:, q]
+            target = acts[:, q] if d < 2 else last[v0 // QUARTER][:, q]
             nc.scalar.activation(target, sums[q, d][:, :, v0 : v0 + n].rearrange("p r v -> p v r"), SILU)
 
         quantize_weights(W2, 0, nc.vector.tensor_copy, "grouped0")
@@ -130,56 +136,76 @@ def tile_picked_wedgecv_silu_l_kernel(tc, x_words, x_scales, w1, w2, w3_words, w
         for v0, n in HALVES:
             project(W2, 1, v0, n, e[1], nc.scalar.copy)
 
-        early = [fetch(0, 0, T, "early0"), fetch(1, 0, QUARTER, "early1")]
-        quantize_weights(W1, 0, nc.scalar.copy, "shared")
-        early[1] = early[1] + fetch(1, QUARTER, T - QUARTER, "shared")
-        quantize_weights(W1, 1, nc.scalar.copy, "sums0_2")
+        plain = {}
+        plain[0] = fetch(0, 0, HALF, "plain0", False)
+        plain[1] = fetch(1, 0, T, "plain1", True)
+        quantize_weights(W1, 0, nc.vector.tensor_copy, "shared")
+        quantize_weights(W1, 1, nc.vector.tensor_copy, "sums0_1")
+        plain[0] = plain[0] + fetch(0, HALF, HALF, "shared", False)
         for t in range(2):
             for v0, n in HALVES:
                 project(W1, t, v0, n, y[t], nc.scalar.copy)
-        for i, target in ((W2, e), (W1, y)):
+        for t in (2, 3):
             for v0, n in HALVES:
-                for t in (2, 3):
-                    project(i, t, v0, n, target[t], nc.scalar.copy)
+                project(W2, t, v0, n, e[t], nc.scalar.copy, bank=PROJECTION_BANKS + 2 * (t - 2) + v0 // HALF)
+        for t in (2, 3):
+            for v0, n in HALVES:
+                project(W1, t, v0, n, y[t], nc.scalar.copy)
 
-        for q, d in ((0, 1), (0, 2), (1, 0), (1, 1), (1, 2)):
+        for q, d in ((0, 1), (0, 2), (1, 1), (1, 2)):
             sums[q, d] = keep.tile([P, 2, T], F32, name=f"sums{q}_{d}", align_bytes=64)
         for t in range(2):
             for d in (1, 2):
                 for v0, n in HALVES if (t, d) == (0, 1) else ((0, T),):
                     fetch_add(t, d, v0, n)
-        for d in range(3):
+        for d in (1, 2):
             for t in (2, 3):
                 fetch_add(t, d, 0, T)
 
-        turned = keep.tile([P, T // P, P, 2], BF16)
-        for g in range(T // P // 2):
-            bank = psum.tile([P, 2, 2, P], F32, name=f"bank{PROJECTION_BANKS + g}")
-            for s in range(2):
-                b = 2 * g + s
-                for r in range(2):
-                    y_block = y[r][:, P * b : P * (b + 1)]
-                    nc.tensor.matmul(bank[:, s, r, :], y_block, identity[:], start=True, stop=False, is_transpose=True)
-                    nc.tensor.matmul(bank[:, s, r, :], early[r][b], identity[:], start=False, stop=True, is_transpose=True)
-            nc.scalar.activation(turned[:, 2 * g : 2 * g + 2, :, :], bank[:].rearrange("v s r p -> v s p r"), SILU)
-        turned_words = turned[:].rearrange("v b p r -> v (b p r)").bitcast(F32)
-        for v0, n in HALVES:
-            bank = psum.tile([P, HALF], F32, name=f"bank{PROJECTION_BANKS + v0 // HALF}")
-            for c0 in range(0, n, P):
-                nc.tensor.transpose(bank[:, c0 : c0 + P], turned_words[:, v0 + c0 : v0 + c0 + P], identity[:])
-            nc.scalar.copy(out=acts[0][:, 0, v0 : v0 + n, :].rearrange("p v r -> p (v r)").bitcast(F32), in_=bank[:])
-        for q, d in sums:
-            n = T if d < 2 else QUARTER
-            for v0 in range(0, T, n):
-                activate(q, d, v0, n)
+        for t in (2, 3):
+            plain[t] = fetch(t, 0, T, f"plain{t}", True)
+
+        first = {}
+
+        def turned_silu(q, first_bank):
+            turned = keep.tile([P, T // P, P, 2], BF16, name=f"turned{q}")
+            turned_words = turned[:].rearrange("v b p r -> v (b p r)").bitcast(F32)
+            for g in range(T // QUARTER):
+                bank = psum.tile([P, 2, 2, P], F32, name=f"bank{first_bank + g}")
+                for s in range(2):
+                    b = 2 * g + s
+                    for r in range(2):
+                        t = 2 * q + r
+                        y_block = y[t][:, P * b : P * (b + 1)]
+                        nc.tensor.matmul(bank[:, s, r, :], y_block, identity[:], start=True, stop=False, is_transpose=True)
+                        nc.tensor.matmul(bank[:, s, r, :], plain[t][b], identity[:], start=False, stop=True, is_transpose=True)
+                nc.scalar.activation(turned[:, 2 * g : 2 * g + 2, :, :], bank[:].rearrange("v s r p -> v s p r"), SILU)
+            for g in range(T // QUARTER):
+                if q == 0:
+                    first[g] = psum.tile([P, 2, QUARTER], F32, name=f"bank{PROJECTION_BANKS + g}")
+                for s in range(2):
+                    b = 2 * g + s
+                    nc.tensor.transpose(first[g][:, q, P * s : P * (s + 1)], turned_words[:, P * b : P * (b + 1)], identity[:])
+
+        turned_silu(0, PROJECTION_BANKS)
+        activate(0, 1, 0, T)
+        turned_silu(1, 0)
+        activate(1, 1, 0, T)
+        for q, k in ((0, 0), (0, 1), (1, 0), (1, 1), (0, 2), (1, 2), (0, 3), (1, 3)):
+            activate(q, 2, QUARTER * k, QUARTER)
 
         best, z = {}, {}
 
         def max_of_two(span):
             v0, n = SPANS[span]
-            v = slice(v0, v0 + n)
+            g, c0 = divmod(v0, QUARTER)
             best[span] = keep.tile([P, 2, n, 2], BF16, name=f"best{span}", align_bytes=64)
-            nc.vector.tensor_tensor(best[span][:], acts[0][:, :, v, :], acts[1][:, :, v, :], MAX)
+            nc.vector.tensor_tensor(
+                best[span][:].rearrange("p q v r -> p q (v r)"),
+                first[g][:, :, c0 : c0 + n].bitcast(BF16),
+                acts[:, :, v0 : v0 + n, :].rearrange("p q v r -> p q (v r)"),
+                MAX,
+            )
 
         def max_of_three(c):
             v0, n = CHUNKS[c]
@@ -200,7 +226,7 @@ def tile_picked_wedgecv_silu_l_kernel(tc, x_words, x_scales, w1, w2, w3_words, w
             nc.vector.quantize_mx(
                 out=z_codes[:].bitcast(FP8X4), scales=z_plane[:], in_=z[c][:].rearrange("p v q r -> p (v q r)")
             )
-            acc = psum.tile([P, HALF], F32, name=f"bank{c}")
+            acc = psum.tile([P, HALF], F32, name=f"bank{c % PROJECTION_BANKS}")
             for m in range(N // P):
                 cols = slice(P * m, P * (m + 1))
                 nc.tensor.matmul_mx(
@@ -223,14 +249,15 @@ def tile_picked_wedgecv_silu_l_kernel(tc, x_words, x_scales, w1, w2, w3_words, w
         max_of_two(0)
         max_of_two(1)
         max_of_three(0)
-        max_of_three(1)
-        finish(0)
-        max_of_three(2)
-        finish(1)
         max_of_two(2)
+        finish(0)
+        max_of_three(1)
+        max_of_two(3)
+        finish(1)
+        max_of_three(2)
+        max_of_two(4)
         finish(2)
         max_of_three(3)
-        max_of_two(3)
-        finish(3)
         max_of_three(4)
+        finish(3)
         finish(4)

@@ -26,6 +26,7 @@ SPARE = 16
 SPARE_PLAIN = 352
 PER_COLUMN = 16
 W2, W1 = 0, 1
+BANKS = 8
 PROJECTION_BANKS = 4
 
 HALVES = ((0, HALF), (HALF, HALF))
@@ -49,7 +50,7 @@ def tile_picked_wedgecv_silu_l_kernel(tc, x_words, x_scales, w1, w2, w3_words, w
         w3_plane = keep.tile([P, N], U8, align_bytes=64)
         x_codes = [keep.tile([P, HALF], U32, name=f"x_codes{h}", align_bytes=64) for h in range(2)]
         w3_codes = keep.tile([P, N], U32, align_bytes=64)
-        w_raw = [keep.tile([P, PACK, H], F32, name=f"w_raw{i}") for i in (W2, W1)]
+        w_raw = [keep.tile([P, PACK, H], F32, name=f"w_raw{i}", align_bytes=64) for i in (W2, W1)]
         e = [keep.tile([P, T + (SPARE_PLAIN if t == 0 else SPARE)], F32, name=f"e{t}") for t in range(PACK)]
         y = [keep.tile([P, T], F32, name=f"y{t}") for t in range(PACK)]
 
@@ -89,7 +90,7 @@ def tile_picked_wedgecv_silu_l_kernel(tc, x_words, x_scales, w1, w2, w3_words, w
 
         def project(i, t, v0, n, target, copy, bank=None):
             if bank is None:
-                bank = len(projected) % PROJECTION_BANKS
+                bank = len(projected) % BANKS
                 projected.append((i, t, v0))
             acc = psum.tile([P, HALF], F32, name=f"bank{bank}")
             h, c0 = divmod(v0, HALF)
@@ -110,12 +111,11 @@ def tile_picked_wedgecv_silu_l_kernel(tc, x_words, x_scales, w1, w2, w3_words, w
         def neighbours(t, d, v0, n):
             return e[t][:].indirect(lists[d][:, v0 // PER_COLUMN : (v0 + n) // PER_COLUMN])
 
-        def fetch(t, v0, n, tag, on_scalar):
-            picked = keep.tile([P, n], F32, name=tag, align_bytes=64)
+        def fetch(t, v0, n, picked, on_scalar):
             if on_scalar:
-                nc.scalar.activation(picked[:], neighbours(t, 0, v0, n), COPY)
+                nc.scalar.activation(picked, neighbours(t, 0, v0, n), COPY)
             else:
-                nc.vector.tensor_copy(picked[:], neighbours(t, 0, v0, n))
+                nc.vector.tensor_copy(picked, neighbours(t, 0, v0, n))
             return [picked[:, P * b : P * (b + 1)] for b in range(n // P)]
 
         sums = {}
@@ -131,24 +131,18 @@ def tile_picked_wedgecv_silu_l_kernel(tc, x_words, x_scales, w1, w2, w3_words, w
         quantize_weights(W2, 0, nc.vector.tensor_copy, "grouped0")
         quantize_weights(W2, 1, nc.vector.tensor_copy, "grouped1")
         project(W2, 0, 0, HALF, e[0], nc.scalar.copy)
-        project(W2, 0, HALF, QUARTER, e[0], nc.vector.tensor_copy)
-        project(W2, 0, HALF + QUARTER, QUARTER, e[0], nc.vector.tensor_copy)
-        for v0, n in HALVES:
-            project(W2, 1, v0, n, e[1], nc.scalar.copy)
+        project(W2, 0, HALF, HALF, e[0], nc.vector.tensor_copy)
+        for t in range(1, PACK):
+            for v0, n in HALVES:
+                project(W2, t, v0, n, e[t], nc.scalar.copy)
 
         plain = {}
-        plain[0] = fetch(0, 0, HALF, "plain0", False)
-        plain[1] = fetch(1, 0, T, "plain1", True)
-        quantize_weights(W1, 0, nc.vector.tensor_copy, "shared")
-        quantize_weights(W1, 1, nc.vector.tensor_copy, "sums0_1")
-        plain[0] = plain[0] + fetch(0, HALF, HALF, "shared", False)
-        for t in range(2):
-            for v0, n in HALVES:
-                project(W1, t, v0, n, y[t], nc.scalar.copy)
-        for t in (2, 3):
-            for v0, n in HALVES:
-                project(W2, t, v0, n, e[t], nc.scalar.copy, bank=PROJECTION_BANKS + 2 * (t - 2) + v0 // HALF)
-        for t in (2, 3):
+        quantize_weights(W1, 0, nc.vector.tensor_copy, "grouped2")
+        quantize_weights(W1, 1, nc.vector.tensor_copy, "grouped3")
+        after = keep.tile([P, T + HALF], F32, name=f"w_raw{W1}", align_bytes=64)
+        plain[0] = fetch(0, 0, T, after[:, :T], False)
+        plain[1] = fetch(1, 0, HALF, after[:, T:], False)
+        for t in range(PACK):
             for v0, n in HALVES:
                 project(W1, t, v0, n, y[t], nc.scalar.copy)
 
@@ -156,14 +150,14 @@ def tile_picked_wedgecv_silu_l_kernel(tc, x_words, x_scales, w1, w2, w3_words, w
             sums[q, d] = keep.tile([P, 2, T], F32, name=f"sums{q}_{d}", align_bytes=64)
         for t in range(2):
             for d in (1, 2):
-                for v0, n in HALVES if (t, d) == (0, 1) else ((0, T),):
-                    fetch_add(t, d, v0, n)
+                fetch_add(t, d, 0, T)
         for d in (1, 2):
             for t in (2, 3):
                 fetch_add(t, d, 0, T)
 
-        for t in (2, 3):
-            plain[t] = fetch(t, 0, T, f"plain{t}", True)
+        plain[1] = plain[1] + fetch(1, HALF, HALF, keep.tile([P, HALF], F32, name="x_codes0", align_bytes=64)[:], True)
+        plain[2] = fetch(2, 0, T, keep.tile([P, T], F32, name="x_codes1", align_bytes=64)[:], True)
+        plain[3] = fetch(3, 0, T, keep.tile([P, T], F32, name="w_codes1_1", align_bytes=64)[:], True)
 
         first = {}
 

@@ -69,6 +69,11 @@ def tile_picked_wedgecv_silu_l_kernel(tc, x_words, x_scales, w1, w2, w3_words, w
         nc.sync.dma_start(out=w3_codes[:].bitcast(I32), in_=w3_words[0].rearrange("p n t -> p (n t)").bitcast(I32))
         load_scale_rows(nc.sync, w3_plane, w3_scales[0])
 
+        seed = keep.tile([P, 1], F32)
+        nc.vector.memset(seed[:], 0.0)
+        unread = keep.tile([P, 1], F32)
+        nc.scalar.activation(unread[:], seed[:], SILU)
+
         w_codes, w_planes = {}, {}
 
         def quantize_weights(i, q, cast, tag):

@@ -144,9 +144,8 @@ def tile_picked_wedgecv_silu_l_kernel(tc, x_words, x_scales, w1, w2, w3_words, w
         plain = {}
         quantize_weights(W1, 0, nc.vector.tensor_copy, "grouped2")
         quantize_weights(W1, 1, nc.vector.tensor_copy, "grouped3")
-        after = keep.tile([P, T + HALF], F32, name=f"w_raw{W1}", align_bytes=64)
-        plain[0] = fetch(0, 0, T, after[:, :T], False)
-        plain[1] = fetch(1, 0, HALF, after[:, T:], False)
+        after = keep.tile([P, T], F32, name=f"w_raw{W1}", align_bytes=64)
+        plain[0] = fetch(0, 0, T, after[:], False)
         for t in range(PACK):
             for v0, n in HALVES:
                 project(W1, t, v0, n, y[t], nc.scalar.copy)
@@ -160,7 +159,7 @@ def tile_picked_wedgecv_silu_l_kernel(tc, x_words, x_scales, w1, w2, w3_words, w
             for t in (2, 3):
                 fetch_add(t, d, 0, T)
 
-        plain[1] = plain[1] + fetch(1, HALF, HALF, keep.tile([P, HALF], F32, name="x_codes0", align_bytes=64)[:], True)
+        plain[1] = fetch(1, 0, T, keep.tile([P, T], F32, name="x_codes0", align_bytes=64)[:], True)
         plain[2] = fetch(2, 0, T, keep.tile([P, T], F32, name="x_codes1", align_bytes=64)[:], True)
         plain[3] = fetch(3, 0, T, keep.tile([P, T], F32, name="w_codes1_1", align_bytes=64)[:], True)
 

@@ -25,6 +25,7 @@ QUARTER = 256
 SPARE = 16
 SPARE_PLAIN = 352
 PER_COLUMN = 16
+VECTOR_SHARE = 128
 W2, W1 = 0, 1
 BANKS = 8
 PROJECTION_BANKS = 4
@@ -50,18 +51,20 @@ def tile_picked_wedgecv_silu_l_kernel(tc, x_words, x_scales, w1, w2, w3_words, w
         w3_plane = keep.tile([P, N], U8, align_bytes=64)
         x_codes = [keep.tile([P, HALF], U32, name=f"x_codes{h}", align_bytes=64) for h in range(2)]
         w3_codes = keep.tile([P, N], U32, align_bytes=64)
-        w_raw = [keep.tile([P, PACK, H], F32, name=f"w_raw{i}", align_bytes=64) for i in (W2, W1)]
+        w2_raw = keep.tile([P, PACK, H], F32, align_bytes=64)
+        w1_raw = [keep.tile([P, PACK, H // 2], F32, name=f"w1_raw{h}", align_bytes=64) for h in range(2)]
         e = [keep.tile([P, T + (SPARE_PLAIN if t == 0 else SPARE)], F32, name=f"e{t}") for t in range(PACK)]
         y = [keep.tile([P, T], F32, name=f"y{t}") for t in range(PACK)]
 
         x_rows = x_words[0].rearrange("p n t -> p (n t)")
         nc.sync.dma_start(lists[0][:], pos1)
-        nc.sync.dma_start(out=w_raw[W2][:], in_=w2.rearrange("(p j) c -> p j c", j=PACK))
-        load_scale_rows(nc.scalar, x_plane, x_scales[0])
+        nc.sync.dma_start(out=w2_raw[:], in_=w2.rearrange("(p j) c -> p j c", j=PACK))
+        load_scale_rows(nc.sync, x_plane, x_scales[0])
         for h in range(2):
             half_row = x_rows[:, PACK * HALF * h : PACK * HALF * (h + 1)]
             nc.sync.dma_start(out=x_codes[h][:].bitcast(I32), in_=half_row.bitcast(I32))
-        nc.sync.dma_start(out=w_raw[W1][:], in_=w1.rearrange("(p j) c -> p j c", j=PACK))
+            half_columns = w1.rearrange("(p j) c -> p j c", j=PACK)[:, :, H // 2 * h : H // 2 * (h + 1)]
+            nc.sync.dma_start(out=w1_raw[h][:], in_=half_columns)
         nc.sync.dma_start(lists[1][:], pos2)
         nc.sync.dma_start(lists[2][:], pos3)
         identity = keep.tile([P, P], F32)
@@ -76,13 +79,14 @@ def tile_picked_wedgecv_silu_l_kernel(tc, x_words, x_scales, w1, w2, w3_words, w
 
         w_codes, w_planes = {}, {}
 
-        def quantize_weights(i, q, cast, tag):
-            grouped = keep.tile([P, 2, P, PACK], BF16, name=tag, align_bytes=64)
-            cast(
-                out=grouped[:].rearrange("p r m j -> p m j r"),
-                in_=w_raw[i][:].rearrange("p j (m t) -> p m j t", t=PACK)[:, :, :, 2 * q : 2 * q + 2],
+        def cast(engine_copy, raw, q, target, walk):
+            engine_copy(
+                out=target.rearrange("p r m j -> p " + walk),
+                in_=raw[:].rearrange("p j (m s r) -> p s m r j", s=2, r=2)[:, q].rearrange("p m r j -> p " + walk),
             )
-            codes = keep.tile([P, 2 * P], U32, name=f"w_codes{i}_{q}", align_bytes=64)
+
+        def quantize_weights(i, q, grouped, tag):
+            codes = keep.tile([P, 2 * P], U32, name=tag, align_bytes=64)
             plane = keep.tile([P, 2 * P], U8, name=f"w_plane{i}_{q}", align_bytes=64)
             nc.vector.quantize_mx(
                 out=codes[:].bitcast(FP8X4), scales=plane[:], in_=grouped[:].rearrange("p r m j -> p (r m j)")
@@ -130,25 +134,36 @@ def tile_picked_wedgecv_silu_l_kernel(tc, x_words, x_scales, w1, w2, w3_words, w
             nc.vector.tensor_tensor(target, neighbours(t, d, v0, n), y[t][:, v0 : v0 + n], ADD)
 
         def activate(q, d, v0, n):
-            target = acts[:, q] if d < 2 else last[v0 // QUARTER][:, q]
+            target = acts[:, q, v0 : v0 + n] if d < 2 else last[v0 // QUARTER][:, q, v0 % QUARTER : v0 % QUARTER + n]
             nc.scalar.activation(target, sums[q, d][:, :, v0 : v0 + n].rearrange("p r v -> p v r"), SILU)
 
-        quantize_weights(W2, 0, nc.vector.tensor_copy, "grouped0")
-        quantize_weights(W2, 1, nc.vector.tensor_copy, "grouped1")
+        grouped = {(i, q): keep.tile([P, 2, P, PACK], BF16, name=f"grouped{i}_{q}", align_bytes=64) for i in (W2, W1) for q in range(2)}
+        cast(nc.vector.tensor_copy, w2_raw, 0, grouped[W2, 0][:], "m j r")
+        cast(nc.scalar.copy, w2_raw, 1, grouped[W2, 1][:], "m r j")
+        quantize_weights(W2, 0, grouped[W2, 0], "w_codes0_0")
+        for q in range(2):
+            cast(nc.vector.tensor_copy, w1_raw[0], q, grouped[W1, q][:, :, : P // 2, :], "m j r")
+        quantize_weights(W2, 1, grouped[W2, 1], "w1_raw0")
         project(W2, 0, 0, HALF, e[0], nc.scalar.copy)
-        project(W2, 0, HALF, HALF, e[0], nc.vector.tensor_copy)
+        project(W2, 0, HALF, QUARTER, e[0], nc.vector.tensor_copy)
+        project(W2, 0, HALF + QUARTER, QUARTER, e[0], nc.vector.tensor_copy, bank=BANKS - 1)
         for t in range(1, PACK):
-            for v0, n in HALVES:
+            for v0, n in HALVES[: 1 if t == PACK - 1 else 2]:
                 project(W2, t, v0, n, e[t], nc.scalar.copy)
 
         plain = {}
-        quantize_weights(W1, 0, nc.vector.tensor_copy, "grouped2")
-        quantize_weights(W1, 1, nc.vector.tensor_copy, "grouped3")
-        after = keep.tile([P, T], F32, name=f"w_raw{W1}", align_bytes=64)
-        plain[0] = fetch(0, 0, T, after[:], False)
+        for q in range(2):
+            cast(nc.vector.tensor_copy, w1_raw[1], q, grouped[W1, q][:, :, P // 2 :, :], "m j r")
+        for q in range(2):
+            quantize_weights(W1, q, grouped[W1, q], f"w_codes1_{q}")
+        after = keep.tile([P, T + VECTOR_SHARE], F32, name="w1_raw1", align_bytes=64)
+        plain[0] = fetch(0, 0, T, after[:, :T], False)
+        plain[1] = fetch(1, 0, VECTOR_SHARE, after[:, T:], False)
         for t in range(PACK):
             for v0, n in HALVES:
                 project(W1, t, v0, n, y[t], nc.scalar.copy)
+            if t == 0:
+                project(W2, PACK - 1, HALF, HALF, e[PACK - 1], nc.scalar.copy, bank=BANKS - 1)
 
         for q, d in ((0, 1), (0, 2), (1, 1), (1, 2)):
             sums[q, d] = keep.tile([P, 2, T], F32, name=f"sums{q}_{d}", align_bytes=64)
@@ -159,7 +174,8 @@ def tile_picked_wedgecv_silu_l_kernel(tc, x_words, x_scales, w1, w2, w3_words, w
             for t in (2, 3):
                 fetch_add(t, d, 0, T)
 
-        plain[1] = fetch(1, 0, T, keep.tile([P, T], F32, name="x_codes0", align_bytes=64)[:], True)
+        rest = keep.tile([P, T - VECTOR_SHARE], F32, name="x_codes0", align_bytes=64)
+        plain[1] = plain[1] + fetch(1, VECTOR_SHARE, T - VECTOR_SHARE, rest[:], True)
         plain[2] = fetch(2, 0, T, keep.tile([P, T], F32, name="x_codes1", align_bytes=64)[:], True)
         plain[3] = fetch(3, 0, T, keep.tile([P, T], F32, name="w_codes1_1", align_bytes=64)[:], True)
 
@@ -188,9 +204,13 @@ def tile_picked_wedgecv_silu_l_kernel(tc, x_words, x_scales, w1, w2, w3_words, w
         turned_silu(0, PROJECTION_BANKS)
         activate(0, 1, 0, T)
         turned_silu(1, 0)
-        activate(1, 1, 0, T)
-        for q, k in ((0, 0), (0, 1), (1, 0), (1, 1), (0, 2), (1, 2), (0, 3), (1, 3)):
+        activate(1, 1, 0, T - QUARTER)
+        for q, k in ((0, 0), (0, 1), (1, 0), (1, 1), (0, 2), (1, 2)):
             activate(q, 2, QUARTER * k, QUARTER)
+        activate(1, 1, T - QUARTER, QUARTER)
+        activate(0, 2, T - QUARTER, QUARTER)
+        for v0, n in CHUNKS[3:]:
+            activate(1, 2, v0, n)
 
         best, z = {}, {}
 
@@ -237,24 +257,23 @@ def tile_picked_wedgecv_silu_l_kernel(tc, x_words, x_scales, w1, w2, w3_words, w
                     stop=True,
                 )
             result = keep.tile([P, 2 * n], F32, name=f"result{c}")
-            copy = nc.vector.tensor_copy if c == len(CHUNKS) - 1 else nc.scalar.copy
+            copy = nc.vector.tensor_copy if c >= len(CHUNKS) - 2 else nc.scalar.copy
             copy(out=result[:], in_=acc[:, : 2 * n])
             nc.sync.dma_start(
                 out=out.rearrange("(m p) v -> p m v", p=P)[:, :, v0 : v0 + n],
                 in_=result[:].rearrange("p (m v) -> p m v", m=2),
             )
 
-        max_of_two(0)
-        max_of_two(1)
+        for c in range(3):
+            max_of_two(c)
         max_of_three(0)
-        max_of_two(2)
-        finish(0)
         max_of_three(1)
-        max_of_two(3)
+        finish(0)
         finish(1)
         max_of_three(2)
-        max_of_two(4)
+        max_of_two(3)
         finish(2)
+        max_of_two(4)
         max_of_three(3)
         max_of_three(4)
         finish(3)

from contextlib import ExitStack

import concourse.mybir as mybir
from concourse.masks import make_identity

K, T, H, N = 512, 1024, 512, 256
FLOPS = 2 * K * H * T * 2 + 2 * H * N * T

F32 = mybir.dt.float32
BF16 = mybir.dt.bfloat16
I32 = mybir.dt.int32
U32 = mybir.dt.uint32
U16 = mybir.dt.uint16
U8 = mybir.dt.uint8
FP8X4 = mybir.dt.float8_e4m3fn_x4
ADD = mybir.AluOpType.add
MAX = mybir.AluOpType.max
SILU = mybir.ActivationFunctionType.Silu
COPY = mybir.ActivationFunctionType.Copy

P = 128
PACK = 4
HALF = 512
QUARTER = 256
SPARE = 16
SPARE_PLAIN = 352
PER_COLUMN = 16
VECTOR_SHARE = 128
W2, W1 = 0, 1
BANKS = 8
PROJECTION_BANKS = 4

HALVES = ((0, HALF), (HALF, HALF))
SPANS = ((0, 256), (256, 256), (512, 256), (768, 128), (896, 128))
CHUNKS = ((0, 256), (256, 256), (512, 256), (768, 128), (896, 128))


def load_scale_rows(queue, plane, rows):
    for g in range(4):
        queue.dma_start(out=plane[32 * g : 32 * g + 4, :].bitcast(I32), in_=rows[4 * g : 4 * g + 4, :].bitcast(I32))


def tile_picked_wedgecv_silu_l_kernel(tc, x_words, x_scales, w1, w2, w3_words, w3_scales, pos1, pos2, pos3, out):
    nc = tc.nc
    with ExitStack() as ctx:
        keep = ctx.enter_context(tc.tile_pool(name="keep", bufs=1))
        psum = ctx.enter_context(tc.psum_pool(name="psum", bufs=1))

        lists = [keep.tile([P, T // PER_COLUMN], U16, name=f"list{d}") for d in range(3)]
        x_plane = keep.tile([P, T], U8, align_bytes=64)
        w3_plane = keep.tile([P, N], U8, align_bytes=64)
        x_codes = [keep.tile([P, HALF], U32, name=f"x_codes{h}", align_bytes=64) for h in range(2)]
        w3_codes = keep.tile([P, N], U32, align_bytes=64)
        w2_raw = keep.tile([P, PACK, H], F32, align_bytes=64)
        w1_raw = [keep.tile([P, PACK, H // 2], F32, name=f"w1_raw{h}", align_bytes=64) for h in range(2)]
        e = [keep.tile([P, T + (SPARE_PLAIN if t == 0 else SPARE)], F32, name=f"e{t}") for t in range(PACK)]
        y = [keep.tile([P, T], F32, name=f"y{t}") for t in range(PACK)]

        x_rows = x_words[0].rearrange("p n t -> p (n t)")
        nc.sync.dma_start(lists[0][:], pos1)
        nc.sync.dma_start(out=w2_raw[:], in_=w2.rearrange("(p j) c -> p j c", j=PACK))
        load_scale_rows(nc.sync, x_plane, x_scales[0])
        for h in range(2):
            half_row = x_rows[:, PACK * HALF * h : PACK * HALF * (h + 1)]
            nc.sync.dma_start(out=x_codes[h][:].bitcast(I32), in_=half_row.bitcast(I32))
            half_columns = w1.rearrange("(p j) c -> p j c", j=PACK)[:, :, H // 2 * h : H // 2 * (h + 1)]
            nc.sync.dma_start(out=w1_raw[h][:], in_=half_columns)
        nc.sync.dma_start(lists[1][:], pos2)
        nc.sync.dma_start(lists[2][:], pos3)
        identity = keep.tile([P, P], F32)
        make_identity(nc, identity[:])
        nc.sync.dma_start(out=w3_codes[:].bitcast(I32), in_=w3_words[0].rearrange("p n t -> p (n t)").bitcast(I32))
        load_scale_rows(nc.sync, w3_plane, w3_scales[0])

        seed = keep.tile([P, 1], F32)
        nc.vector.memset(seed[:], 0.0)
        unread = keep.tile([P, 1], F32)
        nc.scalar.activation(unread[:], seed[:], SILU)

        w_codes, w_planes = {}, {}

        def cast(engine_copy, raw, q, target, walk):
            engine_copy(
                out=target.rearrange("p r m j -> p " + walk),
                in_=raw[:].rearrange("p j (m s r) -> p s m r j", s=2, r=2)[:, q].rearrange("p m r j -> p " + walk),
            )

        def quantize_weights(i, q, grouped, tag):
            codes = keep.tile([P, 2 * P], U32, name=tag, align_bytes=64)
            plane = keep.tile([P, 2 * P], U8, name=f"w_plane{i}_{q}", align_bytes=64)
            nc.vector.quantize_mx(
                out=codes[:].bitcast(FP8X4), scales=plane[:], in_=grouped[:].rearrange("p r m j -> p (r m j)")
            )
            for r in range(2):
                cols = slice(P * r, P * (r + 1))
                w_codes[i, 2 * q + r], w_planes[i, 2 * q + r] = codes[:, cols], plane[:, cols]

        projected = []

        def project(i, t, v0, n, target, copy, bank=None):
            if bank is None:
                bank = len(projected) % BANKS
                projected.append((i, t, v0))
            acc = psum.tile([P, HALF], F32, name=f"bank{bank}")
            h, c0 = divmod(v0, HALF)
            nc.tensor.matmul_mx(
                out=acc[:, :n],
                lhsT=w_codes[i, t].bitcast(FP8X4),
                lhsT_scale=w_planes[i, t],
                rhs=x_codes[h][:, c0 : c0 + n].bitcast(FP8X4),
                rhs_scale=x_plane[:, v0 : v0 + n],
                start=True,
                stop=True,
            )
            copy(out=target[:, v0 : v0 + n], in_=acc[:, :n])

        acts = keep.tile([P, 2, T, 2], BF16, align_bytes=64)
        last = [keep.tile([P, 2, QUARTER, 2], BF16, name=f"last{k}", align_bytes=64) for k in range(T // QUARTER)]

        def neighbours(t, d, v0, n):
            return e[t][:].indirect(lists[d][:, v0 // PER_COLUMN : (v0 + n) // PER_COLUMN])

        def fetch(t, v0, n, picked, on_scalar):
            if on_scalar:
                nc.scalar.activation(picked, neighbours(t, 0, v0, n), COPY)
            else:
                nc.vector.tensor_copy(picked, neighbours(t, 0, v0, n))
            return [picked[:, P * b : P * (b + 1)] for b in range(n // P)]

        sums = {}

        def fetch_add(t, d, v0, n):
            target = sums[t // 2, d][:, t % 2, v0 : v0 + n]
            nc.vector.tensor_tensor(target, neighbours(t, d, v0, n), y[t][:, v0 : v0 + n], ADD)

        def activate(q, d, v0, n):
            target = acts[:, q, v0 : v0 + n] if d < 2 else last[v0 // QUARTER][:, q, v0 % QUARTER : v0 % QUARTER + n]
            nc.scalar.activation(target, sums[q, d][:, :, v0 : v0 + n].rearrange("p r v -> p v r"), SILU)

        grouped = {(i, q): keep.tile([P, 2, P, PACK], BF16, name=f"grouped{i}_{q}", align_bytes=64) for i in (W2, W1) for q in range(2)}
        cast(nc.vector.tensor_copy, w2_raw, 0, grouped[W2, 0][:], "m j r")
        cast(nc.scalar.copy, w2_raw, 1, grouped[W2, 1][:], "m r j")
        quantize_weights(W2, 0, grouped[W2, 0], "w_codes0_0")
        for q in range(2):
            cast(nc.vector.tensor_copy, w1_raw[0], q, grouped[W1, q][:, :, : P // 2, :], "m j r")
        quantize_weights(W2, 1, grouped[W2, 1], "w1_raw0")
        project(W2, 0, 0, HALF, e[0], nc.scalar.copy)
        project(W2, 0, HALF, QUARTER, e[0], nc.vector.tensor_copy)
        project(W2, 0, HALF + QUARTER, QUARTER, e[0], nc.vector.tensor_copy, bank=BANKS - 1)
        for t in range(1, PACK):
            for v0, n in HALVES[: 1 if t == PACK - 1 else 2]:
                project(W2, t, v0, n, e[t], nc.scalar.copy)

        plain = {}
        for q in range(2):
            cast(nc.vector.tensor_copy, w1_raw[1], q, grouped[W1, q][:, :, P // 2 :, :], "m j r")
        for q in range(2):
            quantize_weights(W1, q, grouped[W1, q], f"w_codes1_{q}")
        after = keep.tile([P, T + VECTOR_SHARE], F32, name="w1_raw1", align_bytes=64)
        plain[0] = fetch(0, 0, T, after[:, :T], False)
        plain[1] = fetch(1, 0, VECTOR_SHARE, after[:, T:], False)
        for t in range(PACK):
            for v0, n in HALVES:
                project(W1, t, v0, n, y[t], nc.scalar.copy)
            if t == 0:
                project(W2, PACK - 1, HALF, HALF, e[PACK - 1], nc.scalar.copy, bank=BANKS - 1)

        for q, d in ((0, 1), (0, 2), (1, 1), (1, 2)):
            sums[q, d] = keep.tile([P, 2, T], F32, name=f"sums{q}_{d}", align_bytes=64)
        for t in range(2):
            for d in (1, 2):
                fetch_add(t, d, 0, T)
        for d in (1, 2):
            for t in (2, 3):
                fetch_add(t, d, 0, T)

        rest = keep.tile([P, T - VECTOR_SHARE], F32, name="x_codes0", align_bytes=64)
        plain[1] = plain[1] + fetch(1, VECTOR_SHARE, T - VECTOR_SHARE, rest[:], True)
        plain[2] = fetch(2, 0, T, keep.tile([P, T], F32, name="x_codes1", align_bytes=64)[:], True)
        plain[3] = fetch(3, 0, T, keep.tile([P, T], F32, name="w_codes1_1", align_bytes=64)[:], True)

        first = {}

        def turned_silu(q, first_bank):
            turned = keep.tile([P, T // P, P, 2], BF16, name=f"turned{q}")
            turned_words = turned[:].rearrange("v b p r -> v (b p r)").bitcast(F32)
            for g in range(T // QUARTER):
                bank = psum.tile([P, 2, 2, P], F32, name=f"bank{first_bank + g}")
                for s in range(2):
                    b = 2 * g + s
                    for r in range(2):
                        t = 2 * q + r
                        y_block = y[t][:, P * b : P * (b + 1)]
                        nc.tensor.matmul(bank[:, s, r, :], y_block, identity[:], start=True, stop=False, is_transpose=True)
                        nc.tensor.matmul(bank[:, s, r, :], plain[t][b], identity[:], start=False, stop=True, is_transpose=True)
                nc.scalar.activation(turned[:, 2 * g : 2 * g + 2, :, :], bank[:].rearrange("v s r p -> v s p r"), SILU)
            for g in range(T // QUARTER):
                if q == 0:
                    first[g] = psum.tile([P, 2, QUARTER], F32, name=f"bank{PROJECTION_BANKS + g}")
                for s in range(2):
                    b = 2 * g + s
                    nc.tensor.transpose(first[g][:, q, P * s : P * (s + 1)], turned_words[:, P * b : P * (b + 1)], identity[:])

        turned_silu(0, PROJECTION_BANKS)
        activate(0, 1, 0, T)
        turned_silu(1, 0)
        activate(1, 1, 0, T - QUARTER)
        for q, k in ((0, 0), (0, 1), (1, 0), (1, 1), (0, 2), (1, 2)):
            activate(q, 2, QUARTER * k, QUARTER)
        activate(1, 1, T - QUARTER, QUARTER)
        activate(0, 2, T - QUARTER, QUARTER)
        for v0, n in CHUNKS[3:]:
            activate(1, 2, v0, n)

        best, z = {}, {}

        def max_of_two(span):
            v0, n = SPANS[span]
            g, c0 = divmod(v0, QUARTER)
            best[span] = keep.tile([P, 2, n, 2], BF16, name=f"best{span}", align_bytes=64)
            nc.vector.tensor_tensor(
                best[span][:].rearrange("p q v r -> p q (v r)"),
                first[g][:, :, c0 : c0 + n].bitcast(BF16),
                acts[:, :, v0 : v0 + n, :].rearrange("p q v r -> p q (v r)"),
                MAX,
            )

        def max_of_three(c):
            v0, n = CHUNKS[c]
            span = max(k for k in range(len(SPANS)) if SPANS[k][0] <= v0)
            c0 = v0 - SPANS[span][0]
            z[c] = keep.tile([P, n, 2, 2], BF16, name=f"z{c}", align_bytes=64)
            nc.vector.tensor_tensor(
                z[c][:],
                best[span][:, :, c0 : c0 + n, :].rearrange("p q v r -> p v q r"),
                last[v0 // QUARTER][:, :, v0 % QUARTER : v0 % QUARTER + n, :].rearrange("p q v r -> p v q r"),
                MAX,
            )

        def finish(c):
            v0, n = CHUNKS[c]
            z_codes = keep.tile([P, n], U32, name=f"z_codes{c}", align_bytes=64)
            z_plane = keep.tile([P, n], U8, name=f"z_plane{c}", align_bytes=64)
            nc.vector.quantize_mx(
                out=z_codes[:].bitcast(FP8X4), scales=z_plane[:], in_=z[c][:].rearrange("p v q r -> p (v q r)")
            )
            acc = psum.tile([P, HALF], F32, name=f"bank{c % PROJECTION_BANKS}")
            for m in range(N // P):
                cols = slice(P * m, P * (m + 1))
                nc.tensor.matmul_mx(
                    out=acc[:, n * m : n * (m + 1)],
                    lhsT=w3_codes[:, cols].bitcast(FP8X4),
                    lhsT_scale=w3_plane[:, cols],
                    rhs=z_codes[:].bitcast(FP8X4),
                    rhs_scale=z_plane[:],
                    start=True,
                    stop=True,
                )
            result = keep.tile([P, 2 * n], F32, name=f"result{c}")
            copy = nc.vector.tensor_copy if c >= len(CHUNKS) - 2 else nc.scalar.copy
            copy(out=result[:], in_=acc[:, : 2 * n])
            nc.sync.dma_start(
                out=out.rearrange("(m p) v -> p m v", p=P)[:, :, v0 : v0 + n],
                in_=result[:].rearrange("p (m v) -> p m v", m=2),
            )

        for c in range(3):
            max_of_two(c)
        max_of_three(0)
        max_of_three(1)
        finish(0)
        finish(1)
        max_of_three(2)
        max_of_two(3)
        finish(2)
        max_of_two(4)
        max_of_three(3)
        max_of_three(4)
        finish(3)
        finish(4)
